import numpy as np
import ml_dtypes


def mxq(x, axis, fmt="e4m3"):
    dtype, down = {"e4m3": (ml_dtypes.float8_e4m3fn, 7), "e5m2": (ml_dtypes.float8_e5m2, 14)}[fmt]
    v = np.moveaxis(np.asarray(x, np.float32).astype(ml_dtypes.bfloat16).astype(np.float64), axis, -1)
    blocks = v.reshape(v.shape[:-1] + (-1, 32))
    amax = np.abs(blocks).max(-1, keepdims=True)
    byte = np.maximum(np.where(amax > 0, np.frexp(amax)[1] - 1 + 127, 0) - down, 1)
    scale = np.exp2(byte - 127.0)
    codes = (blocks / scale).astype(np.float32).astype(dtype).astype(np.float64)
    return np.moveaxis((codes * scale).reshape(v.shape), -1, axis)


WIDE = False


def mx_kscale(k):
    if not WIDE:
        return np.ones(k)
    levels = np.array([10, -10, 5, -5, 0])
    if k % 512:
        return np.exp2(np.random.permutation(np.resize(levels, k // 32))).repeat(32)
    a = np.empty((k // 512, 16))
    for p in range(k // 512):
        a[p, :8] = np.random.permutation(np.resize(levels, 8))
        for g in range(8):
            far = levels[np.abs(levels - a[p, g]) >= 10]
            a[p, g + 8] = far[np.random.randint(len(far))]
    return np.exp2(a.ravel()).repeat(32)


BF16 = ml_dtypes.bfloat16


def bf(x):
    return np.asarray(x, np.float32).astype(BF16)


def f64(x):
    return np.asarray(x).astype(np.float64)


E2M1 = np.array([0.0, 0.5, 1.0, 1.5, 2.0, 3.0, 4.0, 6.0, -0.0, -0.5, -1.0, -1.5, -2.0, -3.0, -4.0, -6.0])


def pack_weight(w, fmt):
    k, n = w.shape
    w = f64(bf(w)).reshape(k // 32, 32, n)
    amax = np.abs(w).max(1)
    if fmt == "e4m3":
        byte = np.frexp(amax)[1] - 1 + 127 - 7
    else:
        mant, ex = np.frexp(amax / 6.0)
        byte = np.where(mant > 0.5, ex, ex - 1) + 127
    byte = np.clip(np.where(amax > 0, byte, 1), 1, 254)
    scaled = (w * np.exp2(127.0 - byte)[:, None, :]).reshape(k, n).astype(np.float32)
    by_word = np.ascontiguousarray(scaled.reshape(k // 512, 128, 4, n).transpose(0, 1, 3, 2))
    if fmt == "e4m3":
        words = by_word.astype(ml_dtypes.float8_e4m3fn).view(np.uint8)
    else:
        c = by_word.astype(ml_dtypes.float4_e2m1fn).view(np.uint8) & 0xF
        words = c[..., 0::2] | (c[..., 1::2] << 4)
    return np.ascontiguousarray(words), np.ascontiguousarray(byte.astype(np.uint8).reshape(k // 512, 16, n))


def unpack_weight(words, scales, fmt):
    g, p, n, _ = words.shape
    if fmt == "e4m3":
        vals = np.ascontiguousarray(words).view(ml_dtypes.float8_e4m3fn).astype(np.float64)
    else:
        nib = np.empty((g, p, n, 4), np.uint8)
        nib[..., 0::2] = words & 0xF
        nib[..., 1::2] = words >> 4
        vals = E2M1[nib]
    vals = vals * np.repeat(np.exp2(scales.astype(np.float64) - 127.0), 8, axis=1)[..., None]
    return vals.transpose(0, 1, 3, 2).reshape(g * 512, n)
def pack4(w):
    words, scales = pack_weight(w, "e2m1")
    return words.reshape(words.shape[0], 128, -1), scales


def unpack4(words, scales):
    return unpack_weight(words.reshape(words.shape[0], 128, -1, 2), scales, "e2m1")


def planes(Y):
    n, m = Y.shape
    b = f64(bf(Y)).reshape(n // 32, 32, m)
    amax = np.abs(b).max(1)
    byte = np.clip(np.where(amax > 0, np.frexp(amax)[1] - 1 + 127 - 7, 1), 1, 254)
    codes = (b * np.exp2(127.0 - byte)[:, None, :]).reshape(n, m).astype(np.float32).astype(ml_dtypes.float8_e4m3fn).view(np.uint8)
    words = codes.reshape(n // 512, 128, 4, m).transpose(0, 1, 3, 2)
    return np.ascontiguousarray(words), np.ascontiguousarray(byte.astype(np.uint8).reshape(n // 512, 16, m))


S, T, D, R = 1024, 1024, 512, 1024


def sketch_features(zq, s1q, s2q, gain):
    z1 = zq @ s1q
    z2 = zq @ s2q
    return z1 * z2 * gain[None, :]


def setup_inputs():
    s, t = mx_kscale(D), mx_kscale(R)
    q = bf(np.random.standard_normal((S, D)) * s)
    k = bf(np.random.standard_normal((T, D)) * s)
    s1_words, s1_scales = pack4(np.random.standard_normal((D, R)) / np.sqrt(D) / s[:, None])
    s2_words, s2_scales = pack4(np.random.standard_normal((D, R)) / np.sqrt(D) / s[:, None])
    return {
        "q": q,
        "k": k,
        "s1_words": s1_words,
        "s1_scales": s1_scales,
        "s2_words": s2_words,
        "s2_scales": s2_scales,
        "gq": bf((1.0 + 0.1 * np.random.standard_normal(R)) * t),
        "gk": bf((1.0 + 0.1 * np.random.standard_normal(R)) / t),
    }


def core(q, k, s1_words, s1_scales, s2_words, s2_scales, gq, gk):
    s1q = unpack4(s1_words, s1_scales)
    s2q = unpack4(s2_words, s2_scales)
    fq = sketch_features(mxq(f64(q), 1, "e4m3"), s1q, s2q, f64(gq))
    fk = sketch_features(mxq(f64(k), 1, "e4m3"), s1q, s2q, f64(gk))
    r = fq.shape[-1]
    c = (mxq(fq, 1, "e4m3") @ mxq(fk, 1, "e4m3").T) / np.sqrt(r)
    n = c * c
    w = n / np.mean(n, axis=1, keepdims=True)
    return w


def reference(q, k, s1_words, s1_scales, s2_words, s2_scales, gq, gk):
    R_out = core(q, k, s1_words, s1_scales, s2_words, s2_scales, gq, gk)
    words, scales = planes(R_out)
    return R_out, words, scales

@@ -1,0 +1,397 @@
+from contextlib import ExitStack
+
+import concourse.mybir as mybir
+from concourse.masks import make_identity
+
+F32 = mybir.dt.float32
+BF16 = mybir.dt.bfloat16
+I32 = mybir.dt.int32
+U32 = mybir.dt.uint32
+U8 = mybir.dt.uint8
+FP8X4 = mybir.dt.float8_e4m3fn_x4
+FP4X4 = mybir.dt.float4_e2m1fn_x4
+ACT = mybir.ActivationFunctionType
+ALU = mybir.AluOpType
+
+FLOPS = 2 * (4 * 1024 * 512 * 1024 + 1024 * 1024 * 1024)
+
+P = 128
+CH = 512
+
+
+def tile_polysketchdegreefourattentionweights_x2_kernel(
+    tc, q, k, s1_words, s1_scales, s2_words, s2_scales, gq, gk, out_0, out_1, out_2
+):
+    nc = tc.nc
+    with ExitStack() as ctx:
+        keep = ctx.enter_context(tc.tile_pool(name="keep", bufs=1))
+        work = ctx.enter_context(tc.tile_pool(name="work", bufs=2))
+        psum = ctx.enter_context(tc.psum_pool(name="psum", bufs=1))
+        ctx.enter_context(tc.manual_schedule())
+
+        rings = {"z1": [0, 1, 2], "z2": [3, 4, 5], "m": [6, 7], "all": [0, 1, 2, 6, 7, 3, 4, 5]}
+        used = {"z1": 0, "z2": 0, "m": 0, "all": 0}
+
+        def bank(kind):
+            ring = rings[kind]
+            i = ring[used[kind] % len(ring)]
+            used[kind] += 1
+            t = psum.tile([P, 512], F32, tag="b%d" % i, name="b%d" % i)
+            return t
+
+        x_raw = []
+        x_grp = []
+        x_cod = []
+        x_scl = []
+        for c in range(4):
+            x_raw.append(keep.tile([P, 4, 512], BF16, tag="xr%d" % c, name="xr%d" % c, align_bytes=64))
+            x_grp.append(keep.tile([P, CH, 4], BF16, tag="xg%d" % c, name="xg%d" % c, align_bytes=64))
+            x_cod.append(keep.tile([P, CH], U32, tag="xc%d" % c, name="xc%d" % c, align_bytes=64))
+            x_scl.append(keep.tile([P, CH], U8, tag="xs%d" % c, name="xs%d" % c, align_bytes=64))
+        w_raw = keep.tile([P, 2, 512], I32, tag="wr", name="wr", align_bytes=64)
+        w_prm = keep.tile([P, 4096], U8, tag="wp", name="wp", align_bytes=64)
+        s_raw = keep.tile([P, 2, 256], I32, tag="sr", name="sr", align_bytes=64)
+        s_prm = keep.tile([P, 2048], U8, tag="sp", name="sp", align_bytes=64)
+        ident = keep.tile([P, P], F32, tag="id", name="ident", align_bytes=64)
+        g_row = keep.tile([P, 2, P], BF16, tag="gr", name="g_row", align_bytes=64)
+        g_rowf = keep.tile([P, 2, P], F32, tag="grf", name="g_rowf", align_bytes=64)
+        g_col = keep.tile([P, 16], F32, tag="gc", name="g_col", align_bytes=64)
+        fk_cod = []
+        fk_scl = []
+        for g in range(2):
+            fk_cod.append(keep.tile([P, 1024], U32, tag="fkc%d" % g, name="fkc%d" % g, align_bytes=64))
+            fk_scl.append(keep.tile([P, 1024], U8, tag="fks%d" % g, name="fks%d" % g, align_bytes=64))
+        fq_cod = {}
+        fq_scl = {}
+        nrm = []
+        o_f = []
+        o_b = []
+        o_cod = []
+        o_scl = []
+        sums = []
+        rcp = []
+        for G in range(2):
+            for g in range(2):
+                n = "fq%d%d" % (G, g)
+                fq_cod[(G, g)] = keep.tile([P, CH], U32, tag=n + "c", name=n + "c", align_bytes=64)
+                fq_scl[(G, g)] = keep.tile([P, CH], U8, tag=n + "s", name=n + "s", align_bytes=64)
+            nrm.append(keep.tile([P, 4, 1024], F32, tag="n%d" % G, name="n%d" % G, align_bytes=64))
+            o_f.append(keep.tile([P, 4, 1024], F32, tag="of%d" % G, name="of%d" % G, align_bytes=64))
+            o_b.append(keep.tile([P, 1024, 4], BF16, tag="ob%d" % G, name="ob%d" % G, align_bytes=64))
+            o_cod.append(keep.tile([P, 1024], U32, tag="oc%d" % G, name="oc%d" % G, align_bytes=64))
+            o_scl.append(keep.tile([P, 1024], U8, tag="os%d" % G, name="os%d" % G, align_bytes=64))
+            sums.append(keep.tile([P, 8], F32, tag="sm%d" % G, name="sm%d" % G, align_bytes=64))
+            rcp.append(keep.tile([P, 8], F32, tag="rc%d" % G, name="rc%d" % G, align_bytes=64))
+
+        is_q = [False, True, False, True]
+        half = [0, 0, 1, 1]
+
+        def x_source(c):
+            rows = slice(512 * half[c], 512 * half[c] + 512)
+            if is_q[c]:
+                return q[rows, :].rearrange("(p t) k -> p t k", t=4)
+            return k[rows, :].rearrange("(j p) k -> p j k", p=P)
+
+        nc.vector.memset(s_raw[:].rearrange("p w n -> p (w n)"), 0)
+        nc.vector.memset(g_row[:].rearrange("p a n -> p (a n)"), 0.0)
+
+        def load_gain(engine, dst, vec, g):
+            engine.dma_start(
+                out=dst.rearrange("t (b i) -> t b i", i=8),
+                in_=vec[512 * g : 512 * g + 512].rearrange("(b t i) -> t b i", t=4, i=8),
+            )
+
+        def load_scales(engine, w, scales):
+            for Q in range(4):
+                engine.dma_start(
+                    out=s_raw[32 * Q : 32 * Q + 4, w, :], in_=scales[0, 4 * Q : 4 * Q + 4, :].bitcast(I32)
+                )
+
+        nc.sync.dma_start(out=x_raw[0][:], in_=x_source(0))
+        nc.sync.dma_start(out=w_raw[:, 0, :], in_=s1_words[0].bitcast(I32))
+        nc.sync.dma_start(out=w_raw[:, 1, :], in_=s2_words[0].bitcast(I32))
+        load_scales(nc.scalar, 0, s1_scales)
+        load_gain(nc.scalar, g_row[0:4, 0, :], gk, 0)
+        make_identity(nc, ident[:])
+        load_scales(nc.gpsimd, 1, s2_scales)
+        load_gain(nc.gpsimd, g_row[4:8, 1, :], gk, 1)
+        load_gain(nc.gpsimd, g_row[8:12, 1, :], gq, 0)
+        load_gain(nc.gpsimd, g_row[12:16, 1, :], gq, 1)
+        for c in range(1, 4):
+            nc.sync.dma_start(out=x_raw[c][:], in_=x_source(c))
+
+        def transposes(c, h):
+            pt = bank("m")
+            words = x_raw[c][:].rearrange("p j k -> p (j k)").bitcast(F32)
+            for j in range(2):
+                for u in range(2):
+                    w0 = 256 * (2 * h + j)
+                    nc.tensor.transpose(
+                        pt[:, 128 * (2 * j + u) : 128 * (2 * j + u) + 128], words[:, w0 + u : w0 + 256 : 2], ident[:]
+                    )
+            return pt
+
+        def x_copy(engine, c, h, pt):
+            dst = x_grp[c][:].rearrange("p n t -> p (n t)").bitcast(F32)[:, 512 * h : 512 * h + 512]
+            dst = dst.rearrange("p (j r u) -> p j r u", j=2, u=2)
+            src = pt[:].rearrange("p (j u r) -> p j r u", j=2, u=2)
+            if engine == "s":
+                nc.scalar.copy(out=dst, in_=src)
+            else:
+                nc.vector.tensor_copy(out=dst, in_=src)
+
+        def x_quant(c, c0, c1):
+            nc.vector.quantize_mx(
+                out=x_cod[c][:, c0:c1].bitcast(FP8X4),
+                scales=x_scl[c][:, c0:c1],
+                in_=x_grp[c][:].rearrange("p n t -> p (n t)")[:, 4 * c0 : 4 * c1],
+            )
+
+        def permute_words(engine, w, g):
+            src = w_raw[:, w, 256 * g : 256 * g + 256].rearrange("p (b t i) -> p t b i", t=4, i=4)
+            o = 256 * (2 * w + g)
+            dst = w_prm[:].bitcast(I32)[:, o : o + 256].rearrange("p (t b i) -> p t b i", t=4, i=4)
+            engine.tensor_copy(out=dst, in_=src)
+
+        def permute_scales(engine, w, g):
+            src = s_raw[:, w, 128 * g : 128 * g + 128].rearrange("p (b t i) -> p t b i", t=4, i=2)
+            o = 128 * (2 * w + g)
+            dst = s_prm[:].bitcast(I32)[:, o : o + 128].rearrange("p (t b i) -> p t b i", t=4, i=2)
+            engine.tensor_copy(out=dst, in_=src)
+
+        def sketch(out, w, g, t, c, c0, c1):
+            col = 128 * (4 * (2 * w + g) + t)
+            nc.tensor.matmul_mx(
+                out=out,
+                lhsT=w_prm[:, 2 * col : 2 * col + 256].bitcast(FP4X4),
+                lhsT_scale=s_prm[:, col : col + 128],
+                rhs=x_cod[c][:, c0:c1].bitcast(FP8X4),
+                rhs_scale=x_scl[c][:, c0:c1],
+                start=True,
+                stop=True,
+            )
+
+        z1g = {}
+        feat = {}
+
+        def gain(u, t):
+            c, g = u // 2, u % 2
+            j = 8 * (1 if is_q[c] else 0) + 4 * g + t
+            return g_col[:, j : j + 1]
+
+        def z1_tiles(u):
+            z1g[u] = work.tile([P, 4, CH], F32, tag="z1g", name="z1g", align_bytes=64, bufs=3)
+            feat[u] = work.tile([P, CH, 4], BF16, tag="feat", name="feat", align_bytes=64, bufs=3)
+
+        def z1_wide(u, t):
+            c, g = u // 2, u % 2
+            if t == 0:
+                z1_tiles(u)
+            b = bank("z1")
+            sketch(b[:], 0, g, t, c, 0, CH)
+            nc.scalar.activation(out=z1g[u][:, t, :], in_=b[:], func=ACT.Copy, scale=gain(u, t))
+
+        def z1_narrow(u, n):
+            c, g = u // 2, u % 2
+            if n == 0:
+                z1_tiles(u)
+            b = bank("z1")
+            for t in range(4):
+                sketch(b[:, 128 * t : 128 * t + 128], 0, g, t, c, 128 * n, 128 * n + 128)
+            for t in range(4):
+                nc.scalar.activation(
+                    out=z1g[u][:, t, 128 * n : 128 * n + 128],
+                    in_=b[:, 128 * t : 128 * t + 128],
+                    func=ACT.Copy,
+                    scale=gain(u, t),
+                )
+
+        def z2_mult(u, n):
+            c, g = u // 2, u % 2
+            b = bank("z2")
+            cols = slice(128 * n, 128 * n + 128)
+            for t in range(4):
+                sketch(b[:, 128 * t : 128 * t + 128], 1, g, t, c, 128 * n, 128 * n + 128)
+            nc.vector.tensor_tensor(
+                out=feat[u][:, cols, :],
+                in0=b[:].rearrange("p (t n) -> p n t", t=4),
+                in1=z1g[u][:, :, cols].rearrange("p t n -> p n t"),
+                op=ALU.mult,
+            )
+
+        def f_quant(u, c0, c1):
+            c, g = u // 2, u % 2
+            if is_q[c]:
+                cod, scl, o = fq_cod[(half[c], g)], fq_scl[(half[c], g)], 0
+            else:
+                cod, scl, o = fk_cod[g], fk_scl[g], 512 * half[c]
+            nc.vector.quantize_mx(
+                out=cod[:, o + c0 : o + c1].bitcast(FP8X4),
+                scales=scl[:, o + c0 : o + c1],
+                in_=feat[u][:].rearrange("p n t -> p (n t)")[:, 4 * c0 : 4 * c1],
+            )
+
+        def stage2(G, t, h, kind):
+            b = bank(kind)
+            rows = slice(128 * t, 128 * t + 128)
+            cols = slice(512 * h, 512 * h + 512)
+            for g in range(2):
+                nc.tensor.matmul_mx(
+                    out=b[:],
+                    lhsT=fq_cod[(G, g)][:, rows].bitcast(FP8X4),
+                    lhsT_scale=fq_scl[(G, g)][:, rows],
+                    rhs=fk_cod[g][:, cols].bitcast(FP8X4),
+                    rhs_scale=fk_scl[g][:, cols],
+                    start=(g == 0),
+                    stop=(g == 1),
+                )
+            nc.scalar.activation(
+                out=nrm[G][:, t, cols],
+                in_=b[:],
+                func=ACT.Square,
+                scale=1.0 / 32.0,
+                accum_out=sums[G][:, 4 * h + t : 4 * h + t + 1],
+            )
+
+        def row_factor(G, t0, t1):
+            nc.vector.tensor_tensor(
+                out=rcp[G][:, 4 + t0 : 4 + t1], in0=sums[G][:, t0:t1], in1=sums[G][:, 4 + t0 : 4 + t1], op=ALU.add
+            )
+            nc.vector.reciprocal(out=rcp[G][:, t0:t1], in_=rcp[G][:, 4 + t0 : 4 + t1])
+
+        def row_scale(engine, G, t):
+            engine.tensor_scalar(
+                out=o_f[G][:, t, :],
+                in0=nrm[G][:, t, :],
+                scalar1=rcp[G][:, t : t + 1],
+                scalar2=1024.0,
+                op0=ALU.mult,
+                op1=ALU.mult,
+            )
+            nc.sync.dma_start(
+                out=out_0[512 * G : 512 * G + 512, :].rearrange("(p t) m -> p t m", t=4)[:, t, :], in_=o_f[G][:, t, :]
+            )
+
+        def out_bf16(engine, G, m0, m1):
+            dst = o_b[G][:, m0:m1, :]
+            src = o_f[G][:, :, m0:m1].rearrange("p t m -> p m t")
+            if engine == "s":
+                nc.scalar.copy(out=dst, in_=src)
+            else:
+                nc.vector.tensor_copy(out=dst, in_=src)
+
+        def out_quant(G, m0, m1):
+            nc.vector.quantize_mx(
+                out=o_cod[G][:, m0:m1].bitcast(FP8X4),
+                scales=o_scl[G][:, m0:m1],
+                in_=o_b[G][:].rearrange("p m t -> p (m t)")[:, 4 * m0 : 4 * m1],
+            )
+            nc.sync.dma_start(
+                out=out_1[G].rearrange("p m t -> p (m t)").bitcast(I32)[:, m0:m1], in_=o_cod[G][:, m0:m1].bitcast(I32)
+            )
+
+        def scale_store(G):
+            for Q in range(4):
+                nc.scalar.dma_start(
+                    out=out_2[G, 4 * Q : 4 * Q + 4, :].bitcast(I32), in_=o_scl[G][32 * Q : 32 * Q + 4, :].bitcast(I32)
+                )
+
+        def gain_columns(a, j0, j1):
+            pg = bank("m")
+            nc.tensor.transpose(pg[:, 0:128], g_rowf[:, a, :], ident[:])
+            nc.vector.tensor_copy(out=g_col[:, j0:j1], in_=pg[:, j0:j1])
+
+        pa = transposes(0, 0)
+        x_copy("s", 0, 0, pa)
+        permute_words(nc.vector, 0, 0)
+        permute_scales(nc.vector, 0, 0)
+        pb = transposes(0, 1)
+        x_copy("s", 0, 1, pb)
+        nc.vector.tensor_copy(out=g_rowf[:, 0, :], in_=g_row[:, 0, :])
+        x_quant(0, 0, 256)
+        gain_columns(0, 0, 4)
+        permute_words(nc.vector, 1, 0)
+        x_quant(0, 256, 512)
+        permute_scales(nc.vector, 1, 0)
+        nc.gpsimd.tensor_copy(out=g_rowf[:, 1, :], in_=g_row[:, 1, :])
+        for w in range(2):
+            permute_words(nc.gpsimd, w, 1)
+            permute_scales(nc.gpsimd, w, 1)
+
+        for n in range(4):
+            z1_narrow(0, n)
+            z2_mult(0, n)
+        gain_columns(1, 4, 16)
+        z1_wide(1, 0)
+        z1_wide(1, 1)
+        pa = transposes(1, 0)
+        pb = transposes(1, 1)
+        x_copy("v", 1, 0, pa)
+        x_copy("v", 1, 1, pb)
+        z1_wide(1, 2)
+        z1_wide(1, 3)
+        f_quant(0, 0, 512)
+        x_quant(1, 0, 512)
+
+        s2_at = {
+            (4, 3): [(0, 0, 0)],
+            (5, 1): [(0, 1, 0)],
+            (5, 3): [(0, 2, 0)],
+            (6, 0): [(0, 3, 0)],
+            (6, 2): [(0, 0, 1)],
+            (6, 3): [(0, 1, 1)],
+            (7, 0): [(0, 2, 1)],
+            (7, 1): [(0, 3, 1)],
+        }
+        for u in range(1, 8):
+            for i in range(4):
+                z2_mult(u, i)
+                if u < 7:
+                    z1_wide(u + 1, i)
+                if i == 0 and u > 1:
+                    f_quant(u - 1, 0, 512)
+                if i == 0 and u == 1:
+                    pass
+                if u in (2, 4):
+                    c = u // 2 + 1
+                    if i == 1:
+                        pa = transposes(c, 0)
+                        pb = transposes(c, 1)
+                        x_copy("s", c, 0, pa)
+                    if i == 2:
+                        x_copy("s", c, 1, pb)
+                    if i == 3:
+                        x_quant(c, 0, 512)
+                for G, t, h in s2_at.get((u, i), []):
+                    stage2(G, t, h, "m")
+                if u == 7 and i > 0:
+                    f_quant(7, 128 * (i - 1), 128 * i)
+                    stage2(1, i - 1, 0, "z1")
+                    stage2(1, i - 1, 1, "z1")
+                if u == 7 and i == 1:
+                    row_factor(0, 0, 2)
+                    row_scale(nc.gpsimd, 0, 0)
+                    row_scale(nc.gpsimd, 0, 1)
+        row_factor(0, 2, 4)
+        row_scale(nc.gpsimd, 0, 2)
+        row_scale(nc.gpsimd, 0, 3)
+        f_quant(7, 384, 512)
+        stage2(1, 3, 0, "m")
+        stage2(1, 3, 1, "m")
+        row_factor(1, 0, 2)
+        row_scale(nc.vector, 1, 0)
+        row_scale(nc.vector, 1, 1)
+        out_bf16("v", 0, 0, 512)
+        out_bf16("v", 0, 512, 1024)
+        out_quant(0, 0, 512)
+        out_quant(0, 512, 1024)
+        row_factor(1, 2, 4)
+        row_scale(nc.vector, 1, 2)
+        row_scale(nc.vector, 1, 3)
+        out_bf16("s", 1, 640, 1024)
+        out_bf16("v", 1, 0, 320)
+        out_bf16("v", 1, 320, 640)
+        out_quant(1, 0, 512)
+        out_quant(1, 512, 1024)
+        scale_store(0)
+        scale_store(1)

@@ -92,6 +92,11 @@ def tile_polysketchdegreefourattentionweights_x2_kernel(
                 return q[rows, :].rearrange("(p t) k -> p t k", t=4)
             return k[rows, :].rearrange("(j p) k -> p j k", p=P)
 
+        warm = keep.tile([P, 512], BF16, tag="warm", name="warm", align_bytes=64)
+        nc.vector.memset(warm[:], 0.0)
+        wb = bank("z1")
+        for n in range(4):
+            nc.tensor.matmul(wb[:], lhsT=warm[:, 0:128], rhs=warm[:], start=True, stop=True)
         nc.vector.memset(s_raw[:].rearrange("p w n -> p (w n)"), 0)
         nc.vector.memset(g_row[:].rearrange("p a n -> p (a n)"), 0.0)
 
@@ -107,17 +112,20 @@ def tile_polysketchdegreefourattentionweights_x2_kernel(
                     out=s_raw[32 * Q : 32 * Q + 4, w, :], in_=scales[0, 4 * Q : 4 * Q + 4, :].bitcast(I32)
                 )
 
-        nc.sync.dma_start(out=x_raw[0][:], in_=x_source(0))
+        src0 = x_source(0)
+        nc.sync.dma_start(out=x_raw[0][:, 0:2, :], in_=src0[:, 0:2, :])
         nc.sync.dma_start(out=w_raw[:, 0, :], in_=s1_words[0].bitcast(I32))
-        nc.sync.dma_start(out=w_raw[:, 1, :], in_=s2_words[0].bitcast(I32))
-        load_scales(nc.scalar, 0, s1_scales)
+        nc.sync.dma_start(out=x_raw[0][:, 2:4, :], in_=src0[:, 2:4, :])
         load_gain(nc.scalar, g_row[0:4, 0, :], gk, 0)
+        load_scales(nc.scalar, 0, s1_scales)
+        nc.sync.dma_start(out=w_raw[:, 1, :], in_=s2_words[0].bitcast(I32))
+        nc.sync.dma_start(out=x_raw[1][:], in_=x_source(1))
+        load_gain(nc.sync, g_row[4:8, 1, :], gk, 1)
+        load_gain(nc.sync, g_row[8:12, 1, :], gq, 0)
+        load_gain(nc.sync, g_row[12:16, 1, :], gq, 1)
         make_identity(nc, ident[:])
         load_scales(nc.gpsimd, 1, s2_scales)
-        load_gain(nc.gpsimd, g_row[4:8, 1, :], gk, 1)
-        load_gain(nc.gpsimd, g_row[8:12, 1, :], gq, 0)
-        load_gain(nc.gpsimd, g_row[12:16, 1, :], gq, 1)
-        for c in range(1, 4):
+        for c in range(2, 4):
             nc.sync.dma_start(out=x_raw[c][:], in_=x_source(c))
 
         def transposes(c, h):
@@ -280,6 +288,14 @@ def tile_polysketchdegreefourattentionweights_x2_kernel(
             else:
                 nc.vector.tensor_copy(out=dst, in_=src)
 
+        def out_pair(engine, G, t0, m0, m1):
+            dst = o_b[G][:, m0:m1, t0 : t0 + 2]
+            src = o_f[G][:, t0 : t0 + 2, m0:m1].rearrange("p t m -> p m t")
+            if engine == "s":
+                nc.scalar.copy(out=dst, in_=src)
+            else:
+                nc.vector.tensor_copy(out=dst, in_=src)
+
         def out_quant(G, m0, m1):
             nc.vector.quantize_mx(
                 out=o_cod[G][:, m0:m1].bitcast(FP8X4),
@@ -297,7 +313,7 @@ def tile_polysketchdegreefourattentionweights_x2_kernel(
                 )
 
         def gain_columns(a, j0, j1):
-            pg = bank("m")
+            pg = bank("z2")
             nc.tensor.transpose(pg[:, 0:128], g_rowf[:, a, :], ident[:])
             nc.vector.tensor_copy(out=g_col[:, j0:j1], in_=pg[:, j0:j1])
 
@@ -308,90 +324,103 @@ def tile_polysketchdegreefourattentionweights_x2_kernel(
         pb = transposes(0, 1)
         x_copy("s", 0, 1, pb)
         nc.vector.tensor_copy(out=g_rowf[:, 0, :], in_=g_row[:, 0, :])
+        permute_words(nc.vector, 0, 1)
+        permute_scales(nc.vector, 0, 1)
         x_quant(0, 0, 256)
         gain_columns(0, 0, 4)
-        permute_words(nc.vector, 1, 0)
         x_quant(0, 256, 512)
+        permute_words(nc.vector, 1, 0)
         permute_scales(nc.vector, 1, 0)
-        nc.gpsimd.tensor_copy(out=g_rowf[:, 1, :], in_=g_row[:, 1, :])
-        for w in range(2):
-            permute_words(nc.gpsimd, w, 1)
-            permute_scales(nc.gpsimd, w, 1)
-
-        for n in range(4):
-            z1_narrow(0, n)
-            z2_mult(0, n)
+        z1_narrow(0, 0)
+        z1_narrow(0, 1)
+        z1_narrow(0, 2)
+        z2_mult(0, 0)
+        nc.vector.tensor_copy(out=g_rowf[:, 1, :], in_=g_row[:, 1, :])
+        permute_words(nc.vector, 1, 1)
+        z1_narrow(0, 3)
+        z2_mult(0, 1)
+        permute_scales(nc.vector, 1, 1)
         gain_columns(1, 4, 16)
-        z1_wide(1, 0)
-        z1_wide(1, 1)
         pa = transposes(1, 0)
         pb = transposes(1, 1)
-        x_copy("v", 1, 0, pa)
+        x_copy("s", 1, 0, pa)
+        z2_mult(0, 2)
+        z1_wide(1, 0)
         x_copy("v", 1, 1, pb)
+        z2_mult(0, 3)
+        x_quant(1, 0, 512)
+        z1_wide(1, 1)
         z1_wide(1, 2)
         z1_wide(1, 3)
         f_quant(0, 0, 512)
-        x_quant(1, 0, 512)
 
         s2_at = {
             (4, 3): [(0, 0, 0)],
             (5, 1): [(0, 1, 0)],
             (5, 3): [(0, 2, 0)],
             (6, 0): [(0, 3, 0)],
-            (6, 2): [(0, 0, 1)],
+            (6, 1): [(0, 0, 1)],
             (6, 3): [(0, 1, 1)],
-            (7, 0): [(0, 2, 1)],
-            (7, 1): [(0, 3, 1)],
         }
-        for u in range(1, 8):
+        for u in range(1, 7):
             for i in range(4):
                 z2_mult(u, i)
-                if u < 7:
-                    z1_wide(u + 1, i)
+                z1_wide(u + 1, i)
                 if i == 0 and u > 1:
                     f_quant(u - 1, 0, 512)
-                if i == 0 and u == 1:
-                    pass
-                if u in (2, 4):
-                    c = u // 2 + 1
+                if u in (1, 3):
+                    c = (u + 3) // 2
                     if i == 1:
                         pa = transposes(c, 0)
-                        pb = transposes(c, 1)
-                        x_copy("s", c, 0, pa)
                     if i == 2:
-                        x_copy("s", c, 1, pb)
+                        x_copy("s", c, 0, pa)
                     if i == 3:
-                        x_quant(c, 0, 512)
+                        pb = transposes(c, 1)
+                        x_copy("s", c, 1, pb)
+                if u in (2, 4) and i == 1:
+                    x_quant(u // 2 + 1, 0, 512)
                 for G, t, h in s2_at.get((u, i), []):
                     stage2(G, t, h, "m")
-                if u == 7 and i > 0:
-                    f_quant(7, 128 * (i - 1), 128 * i)
-                    stage2(1, i - 1, 0, "z1")
-                    stage2(1, i - 1, 1, "z1")
-                if u == 7 and i == 1:
-                    row_factor(0, 0, 2)
-                    row_scale(nc.gpsimd, 0, 0)
-                    row_scale(nc.gpsimd, 0, 1)
+        z2_mult(7, 0)
+        f_quant(6, 0, 512)
+        row_factor(0, 0, 2)
+        row_scale(nc.gpsimd, 0, 0)
+        row_scale(nc.gpsimd, 0, 1)
+        stage2(0, 2, 1, "z1")
+        z2_mult(7, 1)
+        stage2(0, 3, 1, "z1")
+        f_quant(7, 0, 128)
+        z2_mult(7, 2)
+        f_quant(7, 128, 256)
+        z2_mult(7, 3)
+        stage2(1, 0, 0, "z1")
+        stage2(1, 0, 1, "m")
+        stage2(1, 1, 0, "m")
+        stage2(1, 1, 1, "z1")
         row_factor(0, 2, 4)
+        f_quant(7, 256, 384)
         row_scale(nc.gpsimd, 0, 2)
-        row_scale(nc.gpsimd, 0, 3)
         f_quant(7, 384, 512)
+        row_scale(nc.gpsimd, 0, 3)
+        stage2(1, 2, 0, "z1")
+        stage2(1, 2, 1, "m")
         stage2(1, 3, 0, "m")
-        stage2(1, 3, 1, "m")
-        row_factor(1, 0, 2)
+        stage2(1, 3, 1, "z1")
+        row_factor(1, 0, 1)
         row_scale(nc.vector, 1, 0)
+        row_factor(1, 1, 2)
         row_scale(nc.vector, 1, 1)
+        out_pair("v", 1, 0, 0, 1024)
+        out_bf16("s", 0, 512, 1024)
         out_bf16("v", 0, 0, 512)
-        out_bf16("v", 0, 512, 1024)
-        out_quant(0, 0, 512)
-        out_quant(0, 512, 1024)
         row_factor(1, 2, 4)
+        out_quant(0, 0, 512)
         row_scale(nc.vector, 1, 2)
         row_scale(nc.vector, 1, 3)
-        out_bf16("s", 1, 640, 1024)
-        out_bf16("v", 1, 0, 320)
-        out_bf16("v", 1, 320, 640)
-        out_quant(1, 0, 512)
-        out_quant(1, 512, 1024)
+        out_pair("v", 1, 2, 0, 512)
+        out_quant(0, 512, 1024)
         scale_store(0)
+        out_quant(1, 0, 512)
+        out_pair("v", 1, 2, 512, 1024)
+        out_quant(1, 512, 1024)
         scale_store(1)

@@ -221,9 +221,9 @@ def tile_polysketchdegreefourattentionweights_x2_kernel(
             for t in range(4):
                 sketch(b[:, 128 * t : 128 * t + 128], 1, g, t, c, 128 * n, 128 * n + 128)
             nc.vector.tensor_tensor(
-                out=feat[u][:, cols, :],
-                in0=b[:].rearrange("p (t n) -> p n t", t=4),
-                in1=z1g[u][:, :, cols].rearrange("p t n -> p n t"),
+                out=feat[u][:, cols, :].rearrange("p (c i) t -> p c t i", i=4),
+                in0=b[:].rearrange("p (t c i) -> p c t i", t=4, i=4),
+                in1=z1g[u][:, :, cols].rearrange("p t (c i) -> p c t i", i=4),
                 op=ALU.mult,
             )
 
@@ -281,16 +281,16 @@ def tile_polysketchdegreefourattentionweights_x2_kernel(
             )
 
         def out_bf16(engine, G, m0, m1):
-            dst = o_b[G][:, m0:m1, :]
-            src = o_f[G][:, :, m0:m1].rearrange("p t m -> p m t")
+            dst = o_b[G][:, m0:m1, :].rearrange("p (c i) t -> p c t i", i=4)
+            src = o_f[G][:, :, m0:m1].rearrange("p t (c i) -> p c t i", i=4)
             if engine == "s":
                 nc.scalar.copy(out=dst, in_=src)
             else:
                 nc.vector.tensor_copy(out=dst, in_=src)
 
         def out_pair(engine, G, t0, m0, m1):
-            dst = o_b[G][:, m0:m1, t0 : t0 + 2]
-            src = o_f[G][:, t0 : t0 + 2, m0:m1].rearrange("p t m -> p m t")
+            dst = o_b[G][:, m0:m1, t0 : t0 + 2].rearrange("p (c i) t -> p c t i", i=4)
+            src = o_f[G][:, t0 : t0 + 2, m0:m1].rearrange("p t (c i) -> p c t i", i=4)
             if engine == "s":
                 nc.scalar.copy(out=dst, in_=src)
             else:

@@ -17,6 +17,17 @@ FLOPS = 2 * (4 * 1024 * 512 * 1024 + 1024 * 1024 * 1024)
 
 P = 128
 CH = 512
+LEAD = [3, 5, 6, 5, 5, 5, 6, 6]
+S2_EARLY = [
+    (19, 0, 0, "m"),
+    (20, 1, 0, "m"),
+    (22, 2, 0, "m"),
+    (24, 3, 0, "m"),
+    (26, 0, 1, "m"),
+    (27, 1, 1, "m"),
+    (29, 2, 1, "z1"),
+    (30, 3, 1, "z1"),
+]
 
 
 def tile_polysketchdegreefourattentionweights_x2_kernel(
@@ -64,10 +75,10 @@ def tile_polysketchdegreefourattentionweights_x2_kernel(
         fq_cod = {}
         fq_scl = {}
         nrm = []
+        o_scl = keep.tile([P, 2, 1024], U8, tag="os", name="os", align_bytes=64)
         o_f = []
         o_b = []
         o_cod = []
-        o_scl = []
         sums = []
         rcp = []
         for G in range(2):
@@ -79,7 +90,6 @@ def tile_polysketchdegreefourattentionweights_x2_kernel(
             o_f.append(keep.tile([P, 4, 1024], F32, tag="of%d" % G, name="of%d" % G, align_bytes=64))
             o_b.append(keep.tile([P, 1024, 4], BF16, tag="ob%d" % G, name="ob%d" % G, align_bytes=64))
             o_cod.append(keep.tile([P, 1024], U32, tag="oc%d" % G, name="oc%d" % G, align_bytes=64))
-            o_scl.append(keep.tile([P, 1024], U8, tag="os%d" % G, name="os%d" % G, align_bytes=64))
             sums.append(keep.tile([P, 8], F32, tag="sm%d" % G, name="sm%d" % G, align_bytes=64))
             rcp.append(keep.tile([P, 8], F32, tag="rc%d" % G, name="rc%d" % G, align_bytes=64))
 
@@ -114,17 +124,17 @@ def tile_polysketchdegreefourattentionweights_x2_kernel(
 
         src0 = x_source(0)
         nc.sync.dma_start(out=x_raw[0][:, 0:2, :], in_=src0[:, 0:2, :])
-        nc.sync.dma_start(out=w_raw[:, 0, :], in_=s1_words[0].bitcast(I32))
         nc.sync.dma_start(out=x_raw[0][:, 2:4, :], in_=src0[:, 2:4, :])
-        load_gain(nc.scalar, g_row[0:4, 0, :], gk, 0)
         load_scales(nc.scalar, 0, s1_scales)
-        nc.sync.dma_start(out=w_raw[:, 1, :], in_=s2_words[0].bitcast(I32))
-        nc.sync.dma_start(out=x_raw[1][:], in_=x_source(1))
+        load_gain(nc.sync, g_row[0:4, 0, :], gk, 0)
+        load_scales(nc.sync, 1, s2_scales)
         load_gain(nc.sync, g_row[4:8, 1, :], gk, 1)
         load_gain(nc.sync, g_row[8:12, 1, :], gq, 0)
         load_gain(nc.sync, g_row[12:16, 1, :], gq, 1)
+        nc.gpsimd.dma_start(out=w_raw[:, 0, :], in_=s1_words[0].bitcast(I32))
         make_identity(nc, ident[:])
-        load_scales(nc.gpsimd, 1, s2_scales)
+        nc.gpsimd.dma_start(out=w_raw[:, 1, :], in_=s2_words[0].bitcast(I32))
+        nc.gpsimd.dma_start(out=x_raw[1][:], in_=x_source(1))
         for c in range(2, 4):
             nc.sync.dma_start(out=x_raw[c][:], in_=x_source(c))
 
@@ -178,6 +188,10 @@ def tile_polysketchdegreefourattentionweights_x2_kernel(
                 start=True,
                 stop=True,
             )
+
+        def stage2_pair(G, t, kind0, kind1):
+            stage2(G, t, 0, kind0)
+            stage2(G, t, 1, kind1)
 
         z1g = {}
         feat = {}
@@ -261,10 +275,12 @@ def tile_polysketchdegreefourattentionweights_x2_kernel(
                 accum_out=sums[G][:, 4 * h + t : 4 * h + t + 1],
             )
 
-        def row_factor(G, t0, t1):
+        def row_sum(G, t0, t1):
             nc.vector.tensor_tensor(
                 out=rcp[G][:, 4 + t0 : 4 + t1], in0=sums[G][:, t0:t1], in1=sums[G][:, 4 + t0 : 4 + t1], op=ALU.add
             )
+
+        def row_recip(G, t0, t1):
             nc.vector.reciprocal(out=rcp[G][:, t0:t1], in_=rcp[G][:, 4 + t0 : 4 + t1])
 
         def row_scale(engine, G, t):
@@ -299,17 +315,18 @@ def tile_polysketchdegreefourattentionweights_x2_kernel(
         def out_quant(G, m0, m1):
             nc.vector.quantize_mx(
                 out=o_cod[G][:, m0:m1].bitcast(FP8X4),
-                scales=o_scl[G][:, m0:m1],
+                scales=o_scl[:, G, m0:m1],
                 in_=o_b[G][:].rearrange("p m t -> p (m t)")[:, 4 * m0 : 4 * m1],
             )
             nc.sync.dma_start(
                 out=out_1[G].rearrange("p m t -> p (m t)").bitcast(I32)[:, m0:m1], in_=o_cod[G][:, m0:m1].bitcast(I32)
             )
 
-        def scale_store(G):
+        def scale_store(engine):
             for Q in range(4):
-                nc.scalar.dma_start(
-                    out=out_2[G, 4 * Q : 4 * Q + 4, :].bitcast(I32), in_=o_scl[G][32 * Q : 32 * Q + 4, :].bitcast(I32)
+                engine.dma_start(
+                    out=out_2[:, 4 * Q : 4 * Q + 4, :].rearrange("g q m -> q g m").bitcast(I32),
+                    in_=o_scl[32 * Q : 32 * Q + 4, :, :].bitcast(I32),
                 )
 
         def gain_columns(a, j0, j1):
@@ -331,96 +348,101 @@ def tile_polysketchdegreefourattentionweights_x2_kernel(
         x_quant(0, 256, 512)
         permute_words(nc.vector, 1, 0)
         permute_scales(nc.vector, 1, 0)
-        z1_narrow(0, 0)
-        z1_narrow(0, 1)
-        z1_narrow(0, 2)
-        z2_mult(0, 0)
-        nc.vector.tensor_copy(out=g_rowf[:, 1, :], in_=g_row[:, 1, :])
-        permute_words(nc.vector, 1, 1)
-        z1_narrow(0, 3)
-        z2_mult(0, 1)
-        permute_scales(nc.vector, 1, 1)
-        gain_columns(1, 4, 16)
-        pa = transposes(1, 0)
-        pb = transposes(1, 1)
-        x_copy("s", 1, 0, pa)
-        z2_mult(0, 2)
-        z1_wide(1, 0)
-        x_copy("v", 1, 1, pb)
-        z2_mult(0, 3)
-        x_quant(1, 0, 512)
-        z1_wide(1, 1)
-        z1_wide(1, 2)
-        z1_wide(1, 3)
-        f_quant(0, 0, 512)
+        pend = {}
+        extras = {}
 
-        s2_at = {
-            (4, 3): [(0, 0, 0)],
-            (5, 1): [(0, 1, 0)],
-            (5, 3): [(0, 2, 0)],
-            (6, 0): [(0, 3, 0)],
-            (6, 1): [(0, 0, 1)],
-            (6, 3): [(0, 1, 1)],
-        }
-        for u in range(1, 7):
-            for i in range(4):
-                z2_mult(u, i)
-                z1_wide(u + 1, i)
-                if i == 0 and u > 1:
-                    f_quant(u - 1, 0, 512)
-                if u in (1, 3):
-                    c = (u + 3) // 2
-                    if i == 1:
-                        pa = transposes(c, 0)
-                    if i == 2:
-                        x_copy("s", c, 0, pa)
-                    if i == 3:
-                        pb = transposes(c, 1)
-                        x_copy("s", c, 1, pb)
-                if u in (2, 4) and i == 1:
-                    x_quant(u // 2 + 1, 0, 512)
-                for G, t, h in s2_at.get((u, i), []):
-                    stage2(G, t, h, "m")
-        z2_mult(7, 0)
-        f_quant(6, 0, 512)
-        row_factor(0, 0, 2)
-        row_scale(nc.gpsimd, 0, 0)
-        row_scale(nc.gpsimd, 0, 1)
-        stage2(0, 2, 1, "z1")
-        z2_mult(7, 1)
-        stage2(0, 3, 1, "z1")
-        f_quant(7, 0, 128)
-        z2_mult(7, 2)
-        f_quant(7, 128, 256)
-        z2_mult(7, 3)
-        stage2(1, 0, 0, "z1")
-        stage2(1, 0, 1, "m")
-        stage2(1, 1, 0, "m")
-        stage2(1, 1, 1, "z1")
-        row_factor(0, 2, 4)
-        f_quant(7, 256, 384)
-        row_scale(nc.gpsimd, 0, 2)
+        def at(slot, fn):
+            extras.setdefault(slot, []).append(fn)
+
+        def x_half(c, h, engine, slot, copy_slot):
+            def turn():
+                pend[(c, h)] = transposes(c, h)
+
+            at(slot, turn)
+            at(copy_slot, lambda: x_copy(engine, c, h, pend[(c, h)]))
+
+        def late_gains():
+            nc.vector.tensor_copy(out=g_rowf[:, 1, :], in_=g_row[:, 1, :])
+            gain_columns(1, 4, 16)
+
+        def late_weights():
+            permute_words(nc.vector, 1, 1)
+            permute_scales(nc.vector, 0, 1)
+            permute_scales(nc.vector, 1, 1)
+
+        x_half(1, 0, "s", 1, 1)
+        x_half(1, 1, "v", 1, 2)
+        at(2, lambda: x_quant(1, 0, 512))
+        at(0, late_weights)
+        at(1, late_gains)
+        x_half(2, 0, "s", 7, 7)
+        x_half(2, 1, "s", 3, 6)
+        at(9, lambda: x_quant(2, 0, 512))
+        x_half(3, 0, "s", 13, 13)
+        x_half(3, 1, "s", 9, 10)
+        at(18, lambda: x_quant(3, 0, 512))
+        for u in range(6):
+            at(4 * u + 5, lambda u=u: f_quant(u, 0, 512))
+        for slot, t, h, kind in S2_EARLY:
+            at(slot, lambda t=t, h=h, kind=kind: stage2(0, t, h, kind))
+
+        z1_list = [(0, n) for n in range(4)] + [(u, t) for u in range(1, 8) for t in range(4)]
+
+        def z1_until(limit, state):
+            while state[0] < min(limit, 32):
+                u, i = z1_list[state[0]]
+                if u == 0:
+                    z1_narrow(0, i)
+                else:
+                    z1_wide(u, i)
+                state[0] += 1
+
+        state = [0]
+        for s in range(32):
+            for fn in extras.get(s, []):
+                fn()
+            u, i = s // 4, s % 4
+            z1_until(s + 4 if u == 0 else 4 * u + 4, state)
+            z2_mult(u, i)
+            if u > 0:
+                z1_until(s + LEAD[u] + 1, state)
+            if s == 28:
+                row_sum(0, 0, 2)
+            if s >= 29:
+                f_quant(6, 128 * (s - 29), 128 * (s - 28))
+                f_quant(7, 128 * (s - 29), 128 * (s - 28))
+            if s == 29:
+                row_recip(0, 0, 2)
+                row_scale(nc.gpsimd, 0, 0)
+                row_scale(nc.gpsimd, 0, 1)
+            if s == 30:
+                stage2_pair(1, 0, "m", "m")
+                row_sum(0, 2, 4)
+        row_recip(0, 2, 4)
+        stage2_pair(1, 1, "z1", "z1")
+        f_quant(6, 384, 512)
         f_quant(7, 384, 512)
-        row_scale(nc.gpsimd, 0, 3)
-        stage2(1, 2, 0, "z1")
-        stage2(1, 2, 1, "m")
-        stage2(1, 3, 0, "m")
-        stage2(1, 3, 1, "z1")
-        row_factor(1, 0, 1)
+        stage2_pair(1, 2, "m", "m")
+        stage2_pair(1, 3, "z1", "z1")
+        row_scale(nc.vector, 0, 2)
+        row_scale(nc.vector, 0, 3)
+        row_sum(1, 0, 2)
+        out_bf16("v", 0, 0, 256)
+        row_recip(1, 0, 2)
+        out_bf16("s", 0, 256, 512)
+        out_bf16("s", 0, 512, 1024)
         row_scale(nc.vector, 1, 0)
-        row_factor(1, 1, 2)
         row_scale(nc.vector, 1, 1)
         out_pair("v", 1, 0, 0, 1024)
-        out_bf16("s", 0, 512, 1024)
-        out_bf16("v", 0, 0, 512)
-        row_factor(1, 2, 4)
+        row_sum(1, 2, 4)
         out_quant(0, 0, 512)
+        row_recip(1, 2, 4)
         row_scale(nc.vector, 1, 2)
         row_scale(nc.vector, 1, 3)
-        out_pair("v", 1, 2, 0, 512)
         out_quant(0, 512, 1024)
-        scale_store(0)
+        out_pair("v", 1, 2, 0, 512)
+        out_pair("s", 1, 2, 768, 1024)
+        out_pair("v", 1, 2, 512, 768)
         out_quant(1, 0, 512)
-        out_pair("v", 1, 2, 512, 1024)
         out_quant(1, 512, 1024)
-        scale_store(1)
+        scale_store(nc.scalar)

@@ -10,24 +10,29 @@ U32 = mybir.dt.uint32
 U8 = mybir.dt.uint8
 FP8X4 = mybir.dt.float8_e4m3fn_x4
 FP4X4 = mybir.dt.float4_e2m1fn_x4
-ACT = mybir.ActivationFunctionType
-ALU = mybir.AluOpType
+COPY = mybir.ActivationFunctionType.Copy
+SQUARE = mybir.ActivationFunctionType.Square
+ADD = mybir.AluOpType.add
+MULT = mybir.AluOpType.mult
 
 FLOPS = 2 * (4 * 1024 * 512 * 1024 + 1024 * 1024 * 1024)
 
 P = 128
-CH = 512
-LEAD = [3, 5, 6, 5, 5, 5, 6, 6]
-S2_EARLY = [
-    (19, 0, 0, "m"),
-    (20, 1, 0, "m"),
-    (22, 2, 0, "m"),
-    (24, 3, 0, "m"),
-    (26, 0, 1, "m"),
-    (27, 1, 1, "m"),
-    (29, 2, 1, "z1"),
-    (30, 3, 1, "z1"),
-]
+ROWS = 1024
+FEATURES = 1024
+CHUNK = 512
+PACK = 4
+
+IS_Q = (False, True, False, True)
+HALF = (0, 0, 1, 1)
+
+Z1_LEAD = (3, 5, 6, 5, 4, 5, 6, 6)
+STEPS = 32
+
+TURN_STEPS = {1: (1, 1), 2: (4, 7), 3: (10, 13)}
+QUANTISE_STEP = {1: 2, 2: 9, 3: 18}
+
+SCORE_STEPS = ((20, 20, 22, 24), (28, 28, 29, 30))
 
 
 def tile_polysketchdegreefourattentionweights_x2_kernel(
@@ -36,84 +41,59 @@ def tile_polysketchdegreefourattentionweights_x2_kernel(
     nc = tc.nc
     with ExitStack() as ctx:
         keep = ctx.enter_context(tc.tile_pool(name="keep", bufs=1))
-        work = ctx.enter_context(tc.tile_pool(name="work", bufs=2))
+        work = ctx.enter_context(tc.tile_pool(name="work", bufs=3))
         psum = ctx.enter_context(tc.psum_pool(name="psum", bufs=1))
         ctx.enter_context(tc.manual_schedule())
 
-        rings = {"z1": [0, 1, 2], "z2": [3, 4, 5], "m": [6, 7], "all": [0, 1, 2, 6, 7, 3, 4, 5]}
-        used = {"z1": 0, "z2": 0, "m": 0, "all": 0}
+        rings = {"z1": (0, 1, 2), "z2": (3, 4, 5), "turn": (6, 7)}
+        taken = {"z1": 0, "z2": 0, "turn": 0}
 
-        def bank(kind):
-            ring = rings[kind]
-            i = ring[used[kind] % len(ring)]
-            used[kind] += 1
-            t = psum.tile([P, 512], F32, tag="b%d" % i, name="b%d" % i)
-            return t
+        def bank(ring):
+            number = rings[ring][taken[ring] % len(rings[ring])]
+            taken[ring] += 1
+            acc = psum.tile([P, 512], F32, tag="bank%d" % number, name="bank%d" % number)
+            return acc
 
-        x_raw = []
-        x_grp = []
-        x_cod = []
-        x_scl = []
+        def keep_tile(name, shape, dtype):
+            held = keep.tile(shape, dtype, tag=name, name=name, align_bytes=64)
+            return held
+
+        x_raw, x_grouped, x_codes, x_scales = [], [], [], []
         for c in range(4):
-            x_raw.append(keep.tile([P, 4, 512], BF16, tag="xr%d" % c, name="xr%d" % c, align_bytes=64))
-            x_grp.append(keep.tile([P, CH, 4], BF16, tag="xg%d" % c, name="xg%d" % c, align_bytes=64))
-            x_cod.append(keep.tile([P, CH], U32, tag="xc%d" % c, name="xc%d" % c, align_bytes=64))
-            x_scl.append(keep.tile([P, CH], U8, tag="xs%d" % c, name="xs%d" % c, align_bytes=64))
-        w_raw = keep.tile([P, 2, 512], I32, tag="wr", name="wr", align_bytes=64)
-        w_prm = keep.tile([P, 4096], U8, tag="wp", name="wp", align_bytes=64)
-        s_raw = keep.tile([P, 2, 256], I32, tag="sr", name="sr", align_bytes=64)
-        s_prm = keep.tile([P, 2048], U8, tag="sp", name="sp", align_bytes=64)
-        ident = keep.tile([P, P], F32, tag="id", name="ident", align_bytes=64)
-        g_row = keep.tile([P, 2, P], BF16, tag="gr", name="g_row", align_bytes=64)
-        g_rowf = keep.tile([P, 2, P], F32, tag="grf", name="g_rowf", align_bytes=64)
-        g_col = keep.tile([P, 16], F32, tag="gc", name="g_col", align_bytes=64)
-        fk_cod = []
-        fk_scl = []
-        for g in range(2):
-            fk_cod.append(keep.tile([P, 1024], U32, tag="fkc%d" % g, name="fkc%d" % g, align_bytes=64))
-            fk_scl.append(keep.tile([P, 1024], U8, tag="fks%d" % g, name="fks%d" % g, align_bytes=64))
-        fq_cod = {}
-        fq_scl = {}
-        nrm = []
-        o_scl = keep.tile([P, 2, 1024], U8, tag="os", name="os", align_bytes=64)
-        o_f = []
-        o_b = []
-        o_cod = []
-        sums = []
-        rcp = []
-        for G in range(2):
-            for g in range(2):
-                n = "fq%d%d" % (G, g)
-                fq_cod[(G, g)] = keep.tile([P, CH], U32, tag=n + "c", name=n + "c", align_bytes=64)
-                fq_scl[(G, g)] = keep.tile([P, CH], U8, tag=n + "s", name=n + "s", align_bytes=64)
-            nrm.append(keep.tile([P, 4, 1024], F32, tag="n%d" % G, name="n%d" % G, align_bytes=64))
-            o_f.append(keep.tile([P, 4, 1024], F32, tag="of%d" % G, name="of%d" % G, align_bytes=64))
-            o_b.append(keep.tile([P, 1024, 4], BF16, tag="ob%d" % G, name="ob%d" % G, align_bytes=64))
-            o_cod.append(keep.tile([P, 1024], U32, tag="oc%d" % G, name="oc%d" % G, align_bytes=64))
-            sums.append(keep.tile([P, 8], F32, tag="sm%d" % G, name="sm%d" % G, align_bytes=64))
-            rcp.append(keep.tile([P, 8], F32, tag="rc%d" % G, name="rc%d" % G, align_bytes=64))
-
-        is_q = [False, True, False, True]
-        half = [0, 0, 1, 1]
+            x_raw.append(keep_tile("x_raw%d" % c, [P, 4, 512], BF16))
+            x_grouped.append(keep_tile("x_grouped%d" % c, [P, CHUNK, PACK], BF16))
+            x_codes.append(keep_tile("x_codes%d" % c, [P, CHUNK], U32))
+            x_scales.append(keep_tile("x_scales%d" % c, [P, CHUNK], U8))
+        w_raw = keep_tile("w_raw", [P, 2, 512], I32)
+        w_codes = keep_tile("w_codes", [P, 2 * 2 * FEATURES], U8)
+        s_raw = keep_tile("s_raw", [P, 2, 256], I32)
+        w_scales = keep_tile("w_scales", [P, 2 * FEATURES], U8)
+        identity = keep_tile("identity", [P, P], F32)
+        g_rows = keep_tile("g_rows", [P, 2, P], BF16)
+        g_rows_f32 = keep_tile("g_rows_f32", [P, 2, P], F32)
+        g_columns = keep_tile("g_columns", [P, 16], F32)
+        fk_codes = [keep_tile("fk_codes%d" % g, [P, ROWS], U32) for g in range(2)]
+        fk_scales = [keep_tile("fk_scales%d" % g, [P, ROWS], U8) for g in range(2)]
+        fq_codes = [[keep_tile("fq_codes%d%d" % (G, g), [P, CHUNK], U32) for g in range(2)] for G in range(2)]
+        fq_scales = [[keep_tile("fq_scales%d%d" % (G, g), [P, CHUNK], U8) for g in range(2)] for G in range(2)]
+        squares = [keep_tile("squares%d" % G, [P, PACK, ROWS], F32) for G in range(2)]
+        sums = [keep_tile("sums%d" % G, [P, 8], F32) for G in range(2)]
+        factors = [keep_tile("factors%d" % G, [P, 8], F32) for G in range(2)]
+        o_f32 = [keep_tile("o_f32%d" % G, [P, PACK, ROWS], F32) for G in range(2)]
+        o_grouped = [keep_tile("o_grouped%d" % G, [P, ROWS, PACK], BF16) for G in range(2)]
+        o_codes = [keep_tile("o_codes%d" % G, [P, ROWS], U32) for G in range(2)]
+        o_scales = keep_tile("o_scales", [P, 2, ROWS], U8)
 
         def x_source(c):
-            rows = slice(512 * half[c], 512 * half[c] + 512)
-            if is_q[c]:
-                return q[rows, :].rearrange("(p t) k -> p t k", t=4)
+            rows = slice(CHUNK * HALF[c], CHUNK * HALF[c] + CHUNK)
+            if IS_Q[c]:
+                return q[rows, :].rearrange("(p t) k -> p t k", t=PACK)
             return k[rows, :].rearrange("(j p) k -> p j k", p=P)
 
-        warm = keep.tile([P, 512], BF16, tag="warm", name="warm", align_bytes=64)
-        nc.vector.memset(warm[:], 0.0)
-        wb = bank("z1")
-        for n in range(4):
-            nc.tensor.matmul(wb[:], lhsT=warm[:, 0:128], rhs=warm[:], start=True, stop=True)
-        nc.vector.memset(s_raw[:].rearrange("p w n -> p (w n)"), 0)
-        nc.vector.memset(g_row[:].rearrange("p a n -> p (a n)"), 0.0)
-
-        def load_gain(engine, dst, vec, g):
+        def load_gain(engine, row, vector, g):
             engine.dma_start(
-                out=dst.rearrange("t (b i) -> t b i", i=8),
-                in_=vec[512 * g : 512 * g + 512].rearrange("(b t i) -> t b i", t=4, i=8),
+                out=g_rows[row : row + 4, 0 if row == 0 else 1, :].rearrange("t (b i) -> t b i", i=8),
+                in_=vector[CHUNK * g : CHUNK * g + CHUNK].rearrange("(b t i) -> t b i", t=PACK, i=8),
             )
 
         def load_scales(engine, w, scales):
@@ -122,327 +102,323 @@ def tile_polysketchdegreefourattentionweights_x2_kernel(
                     out=s_raw[32 * Q : 32 * Q + 4, w, :], in_=scales[0, 4 * Q : 4 * Q + 4, :].bitcast(I32)
                 )
 
-        src0 = x_source(0)
-        nc.sync.dma_start(out=x_raw[0][:, 0:2, :], in_=src0[:, 0:2, :])
-        nc.sync.dma_start(out=x_raw[0][:, 2:4, :], in_=src0[:, 2:4, :])
+        nc.vector.memset(g_rows[:].rearrange("p a n -> p (a n)"), 0.0)
+        nc.vector.memset(s_raw[:].rearrange("p w n -> p (w n)"), 0)
+
+        first = x_source(0)
+        nc.sync.dma_start(out=x_raw[0][:, 0:2, :], in_=first[:, 0:2, :])
+        nc.sync.dma_start(out=x_raw[0][:, 2:4, :], in_=first[:, 2:4, :])
+        load_gain(nc.scalar, 0, gk, 0)
         load_scales(nc.scalar, 0, s1_scales)
-        load_gain(nc.sync, g_row[0:4, 0, :], gk, 0)
         load_scales(nc.sync, 1, s2_scales)
-        load_gain(nc.sync, g_row[4:8, 1, :], gk, 1)
-        load_gain(nc.sync, g_row[8:12, 1, :], gq, 0)
-        load_gain(nc.sync, g_row[12:16, 1, :], gq, 1)
+        load_gain(nc.sync, 4, gk, 1)
+        load_gain(nc.sync, 8, gq, 0)
+        load_gain(nc.sync, 12, gq, 1)
         nc.gpsimd.dma_start(out=w_raw[:, 0, :], in_=s1_words[0].bitcast(I32))
-        make_identity(nc, ident[:])
+        make_identity(nc, identity[:])
         nc.gpsimd.dma_start(out=w_raw[:, 1, :], in_=s2_words[0].bitcast(I32))
         nc.gpsimd.dma_start(out=x_raw[1][:], in_=x_source(1))
         for c in range(2, 4):
             nc.sync.dma_start(out=x_raw[c][:], in_=x_source(c))
 
-        def transposes(c, h):
-            pt = bank("m")
+        def turn(c, h):
+            turned = bank("turn")
             words = x_raw[c][:].rearrange("p j k -> p (j k)").bitcast(F32)
             for j in range(2):
+                w0 = 256 * (2 * h + j)
                 for u in range(2):
-                    w0 = 256 * (2 * h + j)
                     nc.tensor.transpose(
-                        pt[:, 128 * (2 * j + u) : 128 * (2 * j + u) + 128], words[:, w0 + u : w0 + 256 : 2], ident[:]
+                        turned[:, 128 * (2 * j + u) : 128 * (2 * j + u) + 128],
+                        words[:, w0 + u : w0 + 256 : 2],
+                        identity[:],
                     )
-            return pt
+            return turned
 
-        def x_copy(engine, c, h, pt):
-            dst = x_grp[c][:].rearrange("p n t -> p (n t)").bitcast(F32)[:, 512 * h : 512 * h + 512]
-            dst = dst.rearrange("p (j r u) -> p j r u", j=2, u=2)
-            src = pt[:].rearrange("p (j u r) -> p j r u", j=2, u=2)
-            if engine == "s":
+        def group(engine, c, h, turned, j0, j1):
+            words = x_grouped[c][:].rearrange("p n t -> p (n t)").bitcast(F32)
+            dst = words[:, 512 * h + 256 * j0 : 512 * h + 256 * j1].rearrange("p (j r u) -> p j r u", r=128, u=2)
+            src = turned[:, 256 * j0 : 256 * j1].rearrange("p (j u r) -> p j r u", u=2, r=128)
+            if engine == "scalar":
                 nc.scalar.copy(out=dst, in_=src)
             else:
                 nc.vector.tensor_copy(out=dst, in_=src)
 
-        def x_quant(c, c0, c1):
+        def quantise_x(c, n0, n1):
             nc.vector.quantize_mx(
-                out=x_cod[c][:, c0:c1].bitcast(FP8X4),
-                scales=x_scl[c][:, c0:c1],
-                in_=x_grp[c][:].rearrange("p n t -> p (n t)")[:, 4 * c0 : 4 * c1],
+                out=x_codes[c][:, n0:n1].bitcast(FP8X4),
+                scales=x_scales[c][:, n0:n1],
+                in_=x_grouped[c][:].rearrange("p n t -> p (n t)")[:, PACK * n0 : PACK * n1],
             )
 
-        def permute_words(engine, w, g):
-            src = w_raw[:, w, 256 * g : 256 * g + 256].rearrange("p (b t i) -> p t b i", t=4, i=4)
+        def order_words(w, g):
             o = 256 * (2 * w + g)
-            dst = w_prm[:].bitcast(I32)[:, o : o + 256].rearrange("p (t b i) -> p t b i", t=4, i=4)
-            engine.tensor_copy(out=dst, in_=src)
+            nc.vector.tensor_copy(
+                out=w_codes[:].bitcast(I32)[:, o : o + 256].rearrange("p (t b i) -> p t b i", t=PACK, i=4),
+                in_=w_raw[:, w, 256 * g : 256 * g + 256].rearrange("p (b t i) -> p t b i", t=PACK, i=4),
+            )
 
-        def permute_scales(engine, w, g):
-            src = s_raw[:, w, 128 * g : 128 * g + 128].rearrange("p (b t i) -> p t b i", t=4, i=2)
+        def order_scales(w, g):
             o = 128 * (2 * w + g)
-            dst = s_prm[:].bitcast(I32)[:, o : o + 128].rearrange("p (t b i) -> p t b i", t=4, i=2)
-            engine.tensor_copy(out=dst, in_=src)
+            nc.vector.tensor_copy(
+                out=w_scales[:].bitcast(I32)[:, o : o + 128].rearrange("p (t b i) -> p t b i", t=PACK, i=2),
+                in_=s_raw[:, w, 128 * g : 128 * g + 128].rearrange("p (b t i) -> p t b i", t=PACK, i=2),
+            )
 
-        def sketch(out, w, g, t, c, c0, c1):
-            col = 128 * (4 * (2 * w + g) + t)
+        def cast_gains(a):
+            nc.vector.tensor_copy(out=g_rows_f32[:, a, :], in_=g_rows[:, a, :])
+
+        def turn_gains(a, j0, j1):
+            turned = bank("z2")
+            nc.tensor.transpose(turned[:, 0:P], g_rows_f32[:, a, :], identity[:])
+            nc.vector.tensor_copy(out=g_columns[:, j0:j1], in_=turned[:, j0:j1])
+
+        def gain(u, t):
+            j = (8 if IS_Q[u // 2] else 0) + 4 * (u % 2) + t
+            return g_columns[:, j : j + 1]
+
+        def sketch(out, w, u, t, n0, n1):
+            c, g = u // 2, u % 2
+            col = P * (4 * (2 * w + g) + t)
             nc.tensor.matmul_mx(
                 out=out,
-                lhsT=w_prm[:, 2 * col : 2 * col + 256].bitcast(FP4X4),
-                lhsT_scale=s_prm[:, col : col + 128],
-                rhs=x_cod[c][:, c0:c1].bitcast(FP8X4),
-                rhs_scale=x_scl[c][:, c0:c1],
+                lhsT=w_codes[:, 2 * col : 2 * col + 2 * P].bitcast(FP4X4),
+                lhsT_scale=w_scales[:, col : col + P],
+                rhs=x_codes[c][:, n0:n1].bitcast(FP8X4),
+                rhs_scale=x_scales[c][:, n0:n1],
                 start=True,
                 stop=True,
             )
 
-        def stage2_pair(G, t, kind0, kind1):
-            stage2(G, t, 0, kind0)
-            stage2(G, t, 1, kind1)
+        z1 = {}
+        feature = {}
 
-        z1g = {}
-        feat = {}
+        def open_unit(u):
+            z1[u] = work.tile([P, PACK, CHUNK], F32, tag="z1", name="z1", align_bytes=64)
+            feature[u] = work.tile([P, CHUNK, PACK], BF16, tag="feature", name="feature", align_bytes=64)
 
-        def gain(u, t):
-            c, g = u // 2, u % 2
-            j = 8 * (1 if is_q[c] else 0) + 4 * g + t
-            return g_col[:, j : j + 1]
-
-        def z1_tiles(u):
-            z1g[u] = work.tile([P, 4, CH], F32, tag="z1g", name="z1g", align_bytes=64, bufs=3)
-            feat[u] = work.tile([P, CH, 4], BF16, tag="feat", name="feat", align_bytes=64, bufs=3)
-
-        def z1_wide(u, t):
-            c, g = u // 2, u % 2
+        def z1_by_slot(u, t):
             if t == 0:
-                z1_tiles(u)
-            b = bank("z1")
-            sketch(b[:], 0, g, t, c, 0, CH)
-            nc.scalar.activation(out=z1g[u][:, t, :], in_=b[:], func=ACT.Copy, scale=gain(u, t))
+                open_unit(u)
+            acc = bank("z1")
+            sketch(acc[:], 0, u, t, 0, CHUNK)
+            nc.scalar.activation(out=z1[u][:, t, :], in_=acc[:], func=COPY, scale=gain(u, t))
 
-        def z1_narrow(u, n):
-            c, g = u // 2, u % 2
+        def z1_by_rows(u, n):
             if n == 0:
-                z1_tiles(u)
-            b = bank("z1")
-            for t in range(4):
-                sketch(b[:, 128 * t : 128 * t + 128], 0, g, t, c, 128 * n, 128 * n + 128)
-            for t in range(4):
+                open_unit(u)
+            acc = bank("z1")
+            for t in range(PACK):
+                sketch(acc[:, P * t : P * t + P], 0, u, t, P * n, P * n + P)
+            for t in range(PACK):
                 nc.scalar.activation(
-                    out=z1g[u][:, t, 128 * n : 128 * n + 128],
-                    in_=b[:, 128 * t : 128 * t + 128],
-                    func=ACT.Copy,
-                    scale=gain(u, t),
+                    out=z1[u][:, t, P * n : P * n + P], in_=acc[:, P * t : P * t + P], func=COPY, scale=gain(u, t)
                 )
 
-        def z2_mult(u, n):
-            c, g = u // 2, u % 2
-            b = bank("z2")
-            cols = slice(128 * n, 128 * n + 128)
-            for t in range(4):
-                sketch(b[:, 128 * t : 128 * t + 128], 1, g, t, c, 128 * n, 128 * n + 128)
+        def multiply(u, n):
+            acc = bank("z2")
+            rows = slice(P * n, P * n + P)
+            for t in range(PACK):
+                sketch(acc[:, P * t : P * t + P], 1, u, t, P * n, P * n + P)
             nc.vector.tensor_tensor(
-                out=feat[u][:, cols, :].rearrange("p (c i) t -> p c t i", i=4),
-                in0=b[:].rearrange("p (t c i) -> p c t i", t=4, i=4),
-                in1=z1g[u][:, :, cols].rearrange("p t (c i) -> p c t i", i=4),
-                op=ALU.mult,
+                out=feature[u][:, rows, :].rearrange("p (c i) t -> p c t i", i=4),
+                in0=acc[:].rearrange("p (t c i) -> p c t i", t=PACK, i=4),
+                in1=z1[u][:, :, rows].rearrange("p t (c i) -> p c t i", i=4),
+                op=MULT,
             )
 
-        def f_quant(u, c0, c1):
+        def quantise_feature(u, n0, n1):
             c, g = u // 2, u % 2
-            if is_q[c]:
-                cod, scl, o = fq_cod[(half[c], g)], fq_scl[(half[c], g)], 0
+            if IS_Q[c]:
+                codes, scales, o = fq_codes[HALF[c]][g], fq_scales[HALF[c]][g], 0
             else:
-                cod, scl, o = fk_cod[g], fk_scl[g], 512 * half[c]
+                codes, scales, o = fk_codes[g], fk_scales[g], CHUNK * HALF[c]
             nc.vector.quantize_mx(
-                out=cod[:, o + c0 : o + c1].bitcast(FP8X4),
-                scales=scl[:, o + c0 : o + c1],
-                in_=feat[u][:].rearrange("p n t -> p (n t)")[:, 4 * c0 : 4 * c1],
+                out=codes[:, o + n0 : o + n1].bitcast(FP8X4),
+                scales=scales[:, o + n0 : o + n1],
+                in_=feature[u][:].rearrange("p n t -> p (n t)")[:, PACK * n0 : PACK * n1],
             )
 
-        def stage2(G, t, h, kind):
-            b = bank(kind)
-            rows = slice(128 * t, 128 * t + 128)
-            cols = slice(512 * h, 512 * h + 512)
+        def score(G, t, h, ring):
+            acc = bank(ring)
+            rows = slice(P * t, P * t + P)
+            keys = slice(CHUNK * h, CHUNK * h + CHUNK)
             for g in range(2):
                 nc.tensor.matmul_mx(
-                    out=b[:],
-                    lhsT=fq_cod[(G, g)][:, rows].bitcast(FP8X4),
-                    lhsT_scale=fq_scl[(G, g)][:, rows],
-                    rhs=fk_cod[g][:, cols].bitcast(FP8X4),
-                    rhs_scale=fk_scl[g][:, cols],
+                    out=acc[:],
+                    lhsT=fq_codes[G][g][:, rows].bitcast(FP8X4),
+                    lhsT_scale=fq_scales[G][g][:, rows],
+                    rhs=fk_codes[g][:, keys].bitcast(FP8X4),
+                    rhs_scale=fk_scales[g][:, keys],
                     start=(g == 0),
                     stop=(g == 1),
                 )
             nc.scalar.activation(
-                out=nrm[G][:, t, cols],
-                in_=b[:],
-                func=ACT.Square,
+                out=squares[G][:, t, keys],
+                in_=acc[:],
+                func=SQUARE,
                 scale=1.0 / 32.0,
                 accum_out=sums[G][:, 4 * h + t : 4 * h + t + 1],
             )
 
-        def row_sum(G, t0, t1):
+        def add_halves(G, t0, t1):
             nc.vector.tensor_tensor(
-                out=rcp[G][:, 4 + t0 : 4 + t1], in0=sums[G][:, t0:t1], in1=sums[G][:, 4 + t0 : 4 + t1], op=ALU.add
+                out=factors[G][:, 4 + t0 : 4 + t1], in0=sums[G][:, t0:t1], in1=sums[G][:, 4 + t0 : 4 + t1], op=ADD
             )
 
-        def row_recip(G, t0, t1):
-            nc.vector.reciprocal(out=rcp[G][:, t0:t1], in_=rcp[G][:, 4 + t0 : 4 + t1])
+        def invert(G, t0, t1):
+            nc.vector.reciprocal(out=factors[G][:, t0:t1], in_=factors[G][:, 4 + t0 : 4 + t1])
 
-        def row_scale(engine, G, t):
+        def normalise(engine, G, t):
             engine.tensor_scalar(
-                out=o_f[G][:, t, :],
-                in0=nrm[G][:, t, :],
-                scalar1=rcp[G][:, t : t + 1],
-                scalar2=1024.0,
-                op0=ALU.mult,
-                op1=ALU.mult,
+                out=o_f32[G][:, t, :],
+                in0=squares[G][:, t, :],
+                scalar1=factors[G][:, t : t + 1],
+                scalar2=float(ROWS),
+                op0=MULT,
+                op1=MULT,
             )
             nc.sync.dma_start(
-                out=out_0[512 * G : 512 * G + 512, :].rearrange("(p t) m -> p t m", t=4)[:, t, :], in_=o_f[G][:, t, :]
+                out=out_0[CHUNK * G : CHUNK * G + CHUNK, :].rearrange("(p t) m -> p t m", t=PACK)[:, t, :],
+                in_=o_f32[G][:, t, :],
             )
 
-        def out_bf16(engine, G, m0, m1):
-            dst = o_b[G][:, m0:m1, :].rearrange("p (c i) t -> p c t i", i=4)
-            src = o_f[G][:, :, m0:m1].rearrange("p t (c i) -> p c t i", i=4)
-            if engine == "s":
+        def group_out(engine, G, t0, t1, m0, m1):
+            dst = o_grouped[G][:, m0:m1, t0:t1].rearrange("p (c i) t -> p c t i", i=4)
+            src = o_f32[G][:, t0:t1, m0:m1].rearrange("p t (c i) -> p c t i", i=4)
+            if engine == "scalar":
                 nc.scalar.copy(out=dst, in_=src)
             else:
                 nc.vector.tensor_copy(out=dst, in_=src)
 
-        def out_pair(engine, G, t0, m0, m1):
-            dst = o_b[G][:, m0:m1, t0 : t0 + 2].rearrange("p (c i) t -> p c t i", i=4)
-            src = o_f[G][:, t0 : t0 + 2, m0:m1].rearrange("p t (c i) -> p c t i", i=4)
-            if engine == "s":
-                nc.scalar.copy(out=dst, in_=src)
-            else:
-                nc.vector.tensor_copy(out=dst, in_=src)
-
-        def out_quant(G, m0, m1):
+        def quantise_out(G, m0, m1):
             nc.vector.quantize_mx(
-                out=o_cod[G][:, m0:m1].bitcast(FP8X4),
-                scales=o_scl[:, G, m0:m1],
-                in_=o_b[G][:].rearrange("p m t -> p (m t)")[:, 4 * m0 : 4 * m1],
+                out=o_codes[G][:, m0:m1].bitcast(FP8X4),
+                scales=o_scales[:, G, m0:m1],
+                in_=o_grouped[G][:].rearrange("p m t -> p (m t)")[:, PACK * m0 : PACK * m1],
             )
             nc.sync.dma_start(
-                out=out_1[G].rearrange("p m t -> p (m t)").bitcast(I32)[:, m0:m1], in_=o_cod[G][:, m0:m1].bitcast(I32)
+                out=out_1[G].rearrange("p m t -> p (m t)").bitcast(I32)[:, m0:m1], in_=o_codes[G][:, m0:m1].bitcast(I32)
             )
 
-        def scale_store(engine):
-            for Q in range(4):
-                engine.dma_start(
-                    out=out_2[:, 4 * Q : 4 * Q + 4, :].rearrange("g q m -> q g m").bitcast(I32),
-                    in_=o_scl[32 * Q : 32 * Q + 4, :, :].bitcast(I32),
+        cast_gains(0)
+        turned = turn(0, 0)
+        group("scalar", 0, 0, turned, 0, 1)
+        group("scalar", 0, 0, turned, 1, 2)
+        order_words(0, 0)
+        quantise_x(0, 0, 128)
+        order_scales(0, 0)
+        turned = turn(0, 1)
+        group("scalar", 0, 1, turned, 0, 2)
+        turn_gains(0, 0, 4)
+        quantise_x(0, 128, 256)
+        order_words(0, 1)
+        quantise_x(0, 256, 512)
+        order_words(1, 0)
+        order_scales(1, 0)
+        cast_gains(1)
+
+        between = {}
+
+        def at(step, work_item):
+            between.setdefault(step, []).append(work_item)
+
+        def order_rest():
+            order_words(1, 1)
+            order_scales(0, 1)
+            order_scales(1, 1)
+
+        turned_halves = {}
+
+        def turn_half(c, h):
+            turned_halves[(c, h)] = turn(c, h)
+
+        def group_half(engine, c, h):
+            group(engine, c, h, turned_halves[(c, h)], 0, 2)
+
+        at(0, order_rest)
+        at(1, lambda: turn_gains(1, 4, 16))
+        for c in (1, 2, 3):
+            for h in range(2):
+                shared = c == 1 and h == 1
+                step = TURN_STEPS[c][h]
+                at(step, lambda c=c, h=h: turn_half(c, h))
+                at(
+                    step + 1 if shared else step,
+                    lambda c=c, h=h, engine="vector" if shared else "scalar": group_half(engine, c, h),
                 )
-
-        def gain_columns(a, j0, j1):
-            pg = bank("z2")
-            nc.tensor.transpose(pg[:, 0:128], g_rowf[:, a, :], ident[:])
-            nc.vector.tensor_copy(out=g_col[:, j0:j1], in_=pg[:, j0:j1])
-
-        pa = transposes(0, 0)
-        x_copy("s", 0, 0, pa)
-        permute_words(nc.vector, 0, 0)
-        permute_scales(nc.vector, 0, 0)
-        pb = transposes(0, 1)
-        x_copy("s", 0, 1, pb)
-        nc.vector.tensor_copy(out=g_rowf[:, 0, :], in_=g_row[:, 0, :])
-        permute_words(nc.vector, 0, 1)
-        permute_scales(nc.vector, 0, 1)
-        x_quant(0, 0, 256)
-        gain_columns(0, 0, 4)
-        x_quant(0, 256, 512)
-        permute_words(nc.vector, 1, 0)
-        permute_scales(nc.vector, 1, 0)
-        pend = {}
-        extras = {}
-
-        def at(slot, fn):
-            extras.setdefault(slot, []).append(fn)
-
-        def x_half(c, h, engine, slot, copy_slot):
-            def turn():
-                pend[(c, h)] = transposes(c, h)
-
-            at(slot, turn)
-            at(copy_slot, lambda: x_copy(engine, c, h, pend[(c, h)]))
-
-        def late_gains():
-            nc.vector.tensor_copy(out=g_rowf[:, 1, :], in_=g_row[:, 1, :])
-            gain_columns(1, 4, 16)
-
-        def late_weights():
-            permute_words(nc.vector, 1, 1)
-            permute_scales(nc.vector, 0, 1)
-            permute_scales(nc.vector, 1, 1)
-
-        x_half(1, 0, "s", 1, 1)
-        x_half(1, 1, "v", 1, 2)
-        at(2, lambda: x_quant(1, 0, 512))
-        at(0, late_weights)
-        at(1, late_gains)
-        x_half(2, 0, "s", 7, 7)
-        x_half(2, 1, "s", 3, 6)
-        at(9, lambda: x_quant(2, 0, 512))
-        x_half(3, 0, "s", 13, 13)
-        x_half(3, 1, "s", 9, 10)
-        at(18, lambda: x_quant(3, 0, 512))
+            at(QUANTISE_STEP[c], lambda c=c: quantise_x(c, 0, CHUNK))
         for u in range(6):
-            at(4 * u + 5, lambda u=u: f_quant(u, 0, 512))
-        for slot, t, h, kind in S2_EARLY:
-            at(slot, lambda t=t, h=h, kind=kind: stage2(0, t, h, kind))
+            at(4 * u + 5, lambda u=u: quantise_feature(u, 0, CHUNK))
+        for h in range(2):
+            for t in range(PACK):
+                ring = "z1" if h == 1 and t >= 2 else "turn"
+                at(SCORE_STEPS[h][t], lambda t=t, h=h, ring=ring: score(0, t, h, ring))
 
-        z1_list = [(0, n) for n in range(4)] + [(u, t) for u in range(1, 8) for t in range(4)]
-
-        def z1_until(limit, state):
-            while state[0] < min(limit, 32):
-                u, i = z1_list[state[0]]
-                if u == 0:
-                    z1_narrow(0, i)
+        def write_z1(written, limit):
+            limit = min(limit, STEPS)
+            for number in range(written, limit):
+                if number < 4:
+                    z1_by_rows(0, number)
                 else:
-                    z1_wide(u, i)
-                state[0] += 1
+                    z1_by_slot(number // 4, number % 4)
+            return max(written, limit)
 
-        state = [0]
-        for s in range(32):
-            for fn in extras.get(s, []):
-                fn()
-            u, i = s // 4, s % 4
-            z1_until(s + 4 if u == 0 else 4 * u + 4, state)
-            z2_mult(u, i)
-            if u > 0:
-                z1_until(s + LEAD[u] + 1, state)
-            if s == 28:
-                row_sum(0, 0, 2)
-            if s >= 29:
-                f_quant(6, 128 * (s - 29), 128 * (s - 28))
-                f_quant(7, 128 * (s - 29), 128 * (s - 28))
-            if s == 29:
-                row_recip(0, 0, 2)
-                row_scale(nc.gpsimd, 0, 0)
-                row_scale(nc.gpsimd, 0, 1)
-            if s == 30:
-                stage2_pair(1, 0, "m", "m")
-                row_sum(0, 2, 4)
-        row_recip(0, 2, 4)
-        stage2_pair(1, 1, "z1", "z1")
-        f_quant(6, 384, 512)
-        f_quant(7, 384, 512)
-        stage2_pair(1, 2, "m", "m")
-        stage2_pair(1, 3, "z1", "z1")
-        row_scale(nc.vector, 0, 2)
-        row_scale(nc.vector, 0, 3)
-        row_sum(1, 0, 2)
-        out_bf16("v", 0, 0, 256)
-        row_recip(1, 0, 2)
-        out_bf16("s", 0, 256, 512)
-        out_bf16("s", 0, 512, 1024)
-        row_scale(nc.vector, 1, 0)
-        row_scale(nc.vector, 1, 1)
-        out_pair("v", 1, 0, 0, 1024)
-        row_sum(1, 2, 4)
-        out_quant(0, 0, 512)
-        row_recip(1, 2, 4)
-        row_scale(nc.vector, 1, 2)
-        row_scale(nc.vector, 1, 3)
-        out_quant(0, 512, 1024)
-        out_pair("v", 1, 2, 0, 512)
-        out_pair("s", 1, 2, 768, 1024)
-        out_pair("v", 1, 2, 512, 768)
-        out_quant(1, 0, 512)
-        out_quant(1, 512, 1024)
-        scale_store(nc.scalar)
+        z1_written = 0
+        for step in range(STEPS):
+            u, n = step // 4, step % 4
+            for work_item in between.get(step, []):
+                work_item()
+            ahead = step + Z1_LEAD[u] + 1
+            z1_written = write_z1(z1_written, ahead if u == 0 else 4 * u + 4)
+            multiply(u, n)
+            z1_written = write_z1(z1_written, ahead)
+            if step == 28:
+                add_halves(0, 0, 2)
+            if step >= 29:
+                done = P * (step - 29)
+                quantise_feature(6, done, done + P)
+                quantise_feature(7, done, done + P)
+            if step == 29:
+                invert(0, 0, 2)
+                normalise(nc.gpsimd, 0, 0)
+                normalise(nc.gpsimd, 0, 1)
+            if step == 30:
+                score(1, 0, 0, "turn")
+                score(1, 0, 1, "turn")
+                add_halves(0, 2, 4)
+
+        split_0, split_1 = 256, 704
+        invert(0, 2, 4)
+        score(1, 1, 0, "z1")
+        score(1, 1, 1, "z1")
+        quantise_feature(6, 384, 512)
+        quantise_feature(7, 384, 512)
+        for t, ring in ((2, "turn"), (3, "z1")):
+            for h in range(2):
+                score(1, t, h, ring)
+        normalise(nc.vector, 0, 2)
+        normalise(nc.vector, 0, 3)
+        add_halves(1, 0, 2)
+        group_out("vector", 0, 0, 4, 0, split_0)
+        invert(1, 0, 2)
+        group_out("scalar", 0, 0, 4, split_0, 512)
+        group_out("scalar", 0, 0, 4, 512, ROWS)
+        normalise(nc.vector, 1, 0)
+        normalise(nc.vector, 1, 1)
+        group_out("vector", 1, 0, 2, 0, ROWS)
+        add_halves(1, 2, 4)
+        quantise_out(0, 0, 512)
+        invert(1, 2, 4)
+        normalise(nc.vector, 1, 2)
+        normalise(nc.vector, 1, 3)
+        quantise_out(0, 512, ROWS)
+        group_out("vector", 1, 2, 4, 0, 512)
+        group_out("scalar", 1, 2, 4, split_1, ROWS)
+        group_out("vector", 1, 2, 4, 512, split_1)
+        quantise_out(1, 0, 512)
+        quantise_out(1, 512, ROWS)
+        for Q in range(4):
+            nc.scalar.dma_start(
+                out=out_2[:, 4 * Q : 4 * Q + 4, :].rearrange("g q m -> q g m").bitcast(I32),
+                in_=o_scales[32 * Q : 32 * Q + 4, :, :].bitcast(I32),
+            )

from contextlib import ExitStack

import concourse.mybir as mybir
from concourse.masks import make_identity

F32 = mybir.dt.float32
BF16 = mybir.dt.bfloat16
I32 = mybir.dt.int32
U32 = mybir.dt.uint32
U8 = mybir.dt.uint8
FP8X4 = mybir.dt.float8_e4m3fn_x4
FP4X4 = mybir.dt.float4_e2m1fn_x4
COPY = mybir.ActivationFunctionType.Copy
SQUARE = mybir.ActivationFunctionType.Square
ADD = mybir.AluOpType.add
MULT = mybir.AluOpType.mult

FLOPS = 2 * (4 * 1024 * 512 * 1024 + 1024 * 1024 * 1024)

P = 128
ROWS = 1024
FEATURES = 1024
CHUNK = 512
PACK = 4

IS_Q = (False, True, False, True)
HALF = (0, 0, 1, 1)

Z1_LEAD = (3, 5, 6, 5, 4, 5, 6, 6)
STEPS = 32

TURN_STEPS = {1: (1, 1), 2: (4, 7), 3: (10, 13)}
QUANTISE_STEP = {1: 2, 2: 9, 3: 18}

SCORE_STEPS = ((20, 20, 22, 24), (28, 28, 29, 30))


def tile_polysketchdegreefourattentionweights_x2_kernel(
    tc, q, k, s1_words, s1_scales, s2_words, s2_scales, gq, gk, out_0, out_1, out_2
):
    nc = tc.nc
    with ExitStack() as ctx:
        keep = ctx.enter_context(tc.tile_pool(name="keep", bufs=1))
        work = ctx.enter_context(tc.tile_pool(name="work", bufs=3))
        psum = ctx.enter_context(tc.psum_pool(name="psum", bufs=1))
        ctx.enter_context(tc.manual_schedule())

        rings = {"z1": (0, 1, 2), "z2": (3, 4, 5), "turn": (6, 7)}
        taken = {"z1": 0, "z2": 0, "turn": 0}

        def bank(ring):
            number = rings[ring][taken[ring] % len(rings[ring])]
            taken[ring] += 1
            acc = psum.tile([P, 512], F32, tag="bank%d" % number, name="bank%d" % number)
            return acc

        def keep_tile(name, shape, dtype):
            held = keep.tile(shape, dtype, tag=name, name=name, align_bytes=64)
            return held

        x_raw, x_grouped, x_codes, x_scales = [], [], [], []
        for c in range(4):
            x_raw.append(keep_tile("x_raw%d" % c, [P, 4, 512], BF16))
            x_grouped.append(keep_tile("x_grouped%d" % c, [P, CHUNK, PACK], BF16))
            x_codes.append(keep_tile("x_codes%d" % c, [P, CHUNK], U32))
            x_scales.append(keep_tile("x_scales%d" % c, [P, CHUNK], U8))
        w_raw = keep_tile("w_raw", [P, 2, 512], I32)
        w_codes = keep_tile("w_codes", [P, 2 * 2 * FEATURES], U8)
        s_raw = keep_tile("s_raw", [P, 2, 256], I32)
        w_scales = keep_tile("w_scales", [P, 2 * FEATURES], U8)
        identity = keep_tile("identity", [P, P], F32)
        g_rows = keep_tile("g_rows", [P, 2, P], BF16)
        g_rows_f32 = keep_tile("g_rows_f32", [P, 2, P], F32)
        g_columns = keep_tile("g_columns", [P, 16], F32)
        fk_codes = [keep_tile("fk_codes%d" % g, [P, ROWS], U32) for g in range(2)]
        fk_scales = [keep_tile("fk_scales%d" % g, [P, ROWS], U8) for g in range(2)]
        fq_codes = [[keep_tile("fq_codes%d%d" % (G, g), [P, CHUNK], U32) for g in range(2)] for G in range(2)]
        fq_scales = [[keep_tile("fq_scales%d%d" % (G, g), [P, CHUNK], U8) for g in range(2)] for G in range(2)]
        squares = [keep_tile("squares%d" % G, [P, PACK, ROWS], F32) for G in range(2)]
        sums = [keep_tile("sums%d" % G, [P, 8], F32) for G in range(2)]
        factors = [keep_tile("factors%d" % G, [P, 8], F32) for G in range(2)]
        o_f32 = [keep_tile("o_f32%d" % G, [P, PACK, ROWS], F32) for G in range(2)]
        o_grouped = [keep_tile("o_grouped%d" % G, [P, ROWS, PACK], BF16) for G in range(2)]
        o_codes = [keep_tile("o_codes%d" % G, [P, ROWS], U32) for G in range(2)]
        o_scales = keep_tile("o_scales", [P, 2, ROWS], U8)

        def x_source(c):
            rows = slice(CHUNK * HALF[c], CHUNK * HALF[c] + CHUNK)
            if IS_Q[c]:
                return q[rows, :].rearrange("(p t) k -> p t k", t=PACK)
            return k[rows, :].rearrange("(j p) k -> p j k", p=P)

        def load_gain(engine, row, vector, g):
            engine.dma_start(
                out=g_rows[row : row + 4, 0 if row == 0 else 1, :].rearrange("t (b i) -> t b i", i=8),
                in_=vector[CHUNK * g : CHUNK * g + CHUNK].rearrange("(b t i) -> t b i", t=PACK, i=8),
            )

        def load_scales(engine, w, scales):
            for Q in range(4):
                engine.dma_start(
                    out=s_raw[32 * Q : 32 * Q + 4, w, :], in_=scales[0, 4 * Q : 4 * Q + 4, :].bitcast(I32)
                )

        nc.vector.memset(g_rows[:].rearrange("p a n -> p (a n)"), 0.0)
        nc.vector.memset(s_raw[:].rearrange("p w n -> p (w n)"), 0)

        first = x_source(0)
        nc.sync.dma_start(out=x_raw[0][:, 0:2, :], in_=first[:, 0:2, :])
        nc.sync.dma_start(out=x_raw[0][:, 2:4, :], in_=first[:, 2:4, :])
        load_gain(nc.scalar, 0, gk, 0)
        load_scales(nc.scalar, 0, s1_scales)
        load_scales(nc.sync, 1, s2_scales)
        load_gain(nc.sync, 4, gk, 1)
        load_gain(nc.sync, 8, gq, 0)
        load_gain(nc.sync, 12, gq, 1)
        nc.gpsimd.dma_start(out=w_raw[:, 0, :], in_=s1_words[0].bitcast(I32))
        make_identity(nc, identity[:])
        nc.gpsimd.dma_start(out=w_raw[:, 1, :], in_=s2_words[0].bitcast(I32))
        nc.gpsimd.dma_start(out=x_raw[1][:], in_=x_source(1))
        for c in range(2, 4):
            nc.sync.dma_start(out=x_raw[c][:], in_=x_source(c))

        def turn(c, h):
            turned = bank("turn")
            words = x_raw[c][:].rearrange("p j k -> p (j k)").bitcast(F32)
            for j in range(2):
                w0 = 256 * (2 * h + j)
                for u in range(2):
                    nc.tensor.transpose(
                        turned[:, 128 * (2 * j + u) : 128 * (2 * j + u) + 128],
                        words[:, w0 + u : w0 + 256 : 2],
                        identity[:],
                    )
            return turned

        def group(engine, c, h, turned, j0, j1):
            words = x_grouped[c][:].rearrange("p n t -> p (n t)").bitcast(F32)
            dst = words[:, 512 * h + 256 * j0 : 512 * h + 256 * j1].rearrange("p (j r u) -> p j r u", r=128, u=2)
            src = turned[:, 256 * j0 : 256 * j1].rearrange("p (j u r) -> p j r u", u=2, r=128)
            if engine == "scalar":
                nc.scalar.copy(out=dst, in_=src)
            else:
                nc.vector.tensor_copy(out=dst, in_=src)

        def quantise_x(c, n0, n1):
            nc.vector.quantize_mx(
                out=x_codes[c][:, n0:n1].bitcast(FP8X4),
                scales=x_scales[c][:, n0:n1],
                in_=x_grouped[c][:].rearrange("p n t -> p (n t)")[:, PACK * n0 : PACK * n1],
            )

        def order_words(w, g):
            o = 256 * (2 * w + g)
            nc.vector.tensor_copy(
                out=w_codes[:].bitcast(I32)[:, o : o + 256].rearrange("p (t b i) -> p t b i", t=PACK, i=4),
                in_=w_raw[:, w, 256 * g : 256 * g + 256].rearrange("p (b t i) -> p t b i", t=PACK, i=4),
            )

        def order_scales(w, g):
            o = 128 * (2 * w + g)
            nc.vector.tensor_copy(
                out=w_scales[:].bitcast(I32)[:, o : o + 128].rearrange("p (t b i) -> p t b i", t=PACK, i=2),
                in_=s_raw[:, w, 128 * g : 128 * g + 128].rearrange("p (b t i) -> p t b i", t=PACK, i=2),
            )

        def cast_gains(a):
            nc.vector.tensor_copy(out=g_rows_f32[:, a, :], in_=g_rows[:, a, :])

        def turn_gains(a, j0, j1):
            turned = bank("z2")
            nc.tensor.transpose(turned[:, 0:P], g_rows_f32[:, a, :], identity[:])
            nc.vector.tensor_copy(out=g_columns[:, j0:j1], in_=turned[:, j0:j1])

        def gain(u, t):
            j = (8 if IS_Q[u // 2] else 0) + 4 * (u % 2) + t
            return g_columns[:, j : j + 1]

        def sketch(out, w, u, t, n0, n1):
            c, g = u // 2, u % 2
            col = P * (4 * (2 * w + g) + t)
            nc.tensor.matmul_mx(
                out=out,
                lhsT=w_codes[:, 2 * col : 2 * col + 2 * P].bitcast(FP4X4),
                lhsT_scale=w_scales[:, col : col + P],
                rhs=x_codes[c][:, n0:n1].bitcast(FP8X4),
                rhs_scale=x_scales[c][:, n0:n1],
                start=True,
                stop=True,
            )

        z1 = {}
        feature = {}

        def open_unit(u):
            z1[u] = work.tile([P, PACK, CHUNK], F32, tag="z1", name="z1", align_bytes=64)
            feature[u] = work.tile([P, CHUNK, PACK], BF16, tag="feature", name="feature", align_bytes=64)

        def z1_by_slot(u, t):
            if t == 0:
                open_unit(u)
            acc = bank("z1")
            sketch(acc[:], 0, u, t, 0, CHUNK)
            nc.scalar.activation(out=z1[u][:, t, :], in_=acc[:], func=COPY, scale=gain(u, t))

        def z1_by_rows(u, n):
            if n == 0:
                open_unit(u)
            acc = bank("z1")
            for t in range(PACK):
                sketch(acc[:, P * t : P * t + P], 0, u, t, P * n, P * n + P)
            for t in range(PACK):
                nc.scalar.activation(
                    out=z1[u][:, t, P * n : P * n + P], in_=acc[:, P * t : P * t + P], func=COPY, scale=gain(u, t)
                )

        def multiply(u, n):
            acc = bank("z2")
            rows = slice(P * n, P * n + P)
            for t in range(PACK):
                sketch(acc[:, P * t : P * t + P], 1, u, t, P * n, P * n + P)
            nc.vector.tensor_tensor(
                out=feature[u][:, rows, :].rearrange("p (c i) t -> p c t i", i=4),
                in0=acc[:].rearrange("p (t c i) -> p c t i", t=PACK, i=4),
                in1=z1[u][:, :, rows].rearrange("p t (c i) -> p c t i", i=4),
                op=MULT,
            )

        def quantise_feature(u, n0, n1):
            c, g = u // 2, u % 2
            if IS_Q[c]:
                codes, scales, o = fq_codes[HALF[c]][g], fq_scales[HALF[c]][g], 0
            else:
                codes, scales, o = fk_codes[g], fk_scales[g], CHUNK * HALF[c]
            nc.vector.quantize_mx(
                out=codes[:, o + n0 : o + n1].bitcast(FP8X4),
                scales=scales[:, o + n0 : o + n1],
                in_=feature[u][:].rearrange("p n t -> p (n t)")[:, PACK * n0 : PACK * n1],
            )

        def score(G, t, h, ring):
            acc = bank(ring)
            rows = slice(P * t, P * t + P)
            keys = slice(CHUNK * h, CHUNK * h + CHUNK)
            for g in range(2):
                nc.tensor.matmul_mx(
                    out=acc[:],
                    lhsT=fq_codes[G][g][:, rows].bitcast(FP8X4),
                    lhsT_scale=fq_scales[G][g][:, rows],
                    rhs=fk_codes[g][:, keys].bitcast(FP8X4),
                    rhs_scale=fk_scales[g][:, keys],
                    start=(g == 0),
                    stop=(g == 1),
                )
            nc.scalar.activation(
                out=squares[G][:, t, keys],
                in_=acc[:],
                func=SQUARE,
                scale=1.0 / 32.0,
                accum_out=sums[G][:, 4 * h + t : 4 * h + t + 1],
            )

        def add_halves(G, t0, t1):
            nc.vector.tensor_tensor(
                out=factors[G][:, 4 + t0 : 4 + t1], in0=sums[G][:, t0:t1], in1=sums[G][:, 4 + t0 : 4 + t1], op=ADD
            )

        def invert(G, t0, t1):
            nc.vector.reciprocal(out=factors[G][:, t0:t1], in_=factors[G][:, 4 + t0 : 4 + t1])

        def normalise(engine, G, t):
            engine.tensor_scalar(
                out=o_f32[G][:, t, :],
                in0=squares[G][:, t, :],
                scalar1=factors[G][:, t : t + 1],
                scalar2=float(ROWS),
                op0=MULT,
                op1=MULT,
            )
            nc.sync.dma_start(
                out=out_0[CHUNK * G : CHUNK * G + CHUNK, :].rearrange("(p t) m -> p t m", t=PACK)[:, t, :],
                in_=o_f32[G][:, t, :],
            )

        def group_out(engine, G, t0, t1, m0, m1):
            dst = o_grouped[G][:, m0:m1, t0:t1].rearrange("p (c i) t -> p c t i", i=4)
            src = o_f32[G][:, t0:t1, m0:m1].rearrange("p t (c i) -> p c t i", i=4)
            if engine == "scalar":
                nc.scalar.copy(out=dst, in_=src)
            else:
                nc.vector.tensor_copy(out=dst, in_=src)

        def quantise_out(G, m0, m1):
            nc.vector.quantize_mx(
                out=o_codes[G][:, m0:m1].bitcast(FP8X4),
                scales=o_scales[:, G, m0:m1],
                in_=o_grouped[G][:].rearrange("p m t -> p (m t)")[:, PACK * m0 : PACK * m1],
            )
            nc.sync.dma_start(
                out=out_1[G].rearrange("p m t -> p (m t)").bitcast(I32)[:, m0:m1], in_=o_codes[G][:, m0:m1].bitcast(I32)
            )

        cast_gains(0)
        turned = turn(0, 0)
        group("scalar", 0, 0, turned, 0, 1)
        group("scalar", 0, 0, turned, 1, 2)
        order_words(0, 0)
        quantise_x(0, 0, 128)
        order_scales(0, 0)
        turned = turn(0, 1)
        group("scalar", 0, 1, turned, 0, 2)
        turn_gains(0, 0, 4)
        quantise_x(0, 128, 256)
        order_words(0, 1)
        quantise_x(0, 256, 512)
        order_words(1, 0)
        order_scales(1, 0)
        cast_gains(1)

        between = {}

        def at(step, work_item):
            between.setdefault(step, []).append(work_item)

        def order_rest():
            order_words(1, 1)
            order_scales(0, 1)
            order_scales(1, 1)

        turned_halves = {}

        def turn_half(c, h):
            turned_halves[(c, h)] = turn(c, h)

        def group_half(engine, c, h):
            group(engine, c, h, turned_halves[(c, h)], 0, 2)

        at(0, order_rest)
        at(1, lambda: turn_gains(1, 4, 16))
        for c in (1, 2, 3):
            for h in range(2):
                shared = c == 1 and h == 1
                step = TURN_STEPS[c][h]
                at(step, lambda c=c, h=h: turn_half(c, h))
                at(
                    step + 1 if shared else step,
                    lambda c=c, h=h, engine="vector" if shared else "scalar": group_half(engine, c, h),
                )
            at(QUANTISE_STEP[c], lambda c=c: quantise_x(c, 0, CHUNK))
        for u in range(6):
            at(4 * u + 5, lambda u=u: quantise_feature(u, 0, CHUNK))
        for h in range(2):
            for t in range(PACK):
                ring = "z1" if h == 1 and t >= 2 else "turn"
                at(SCORE_STEPS[h][t], lambda t=t, h=h, ring=ring: score(0, t, h, ring))

        def write_z1(written, limit):
            limit = min(limit, STEPS)
            for number in range(written, limit):
                if number < 4:
                    z1_by_rows(0, number)
                else:
                    z1_by_slot(number // 4, number % 4)
            return max(written, limit)

        z1_written = 0
        for step in range(STEPS):
            u, n = step // 4, step % 4
            for work_item in between.get(step, []):
                work_item()
            ahead = step + Z1_LEAD[u] + 1
            z1_written = write_z1(z1_written, ahead if u == 0 else 4 * u + 4)
            multiply(u, n)
            z1_written = write_z1(z1_written, ahead)
            if step == 28:
                add_halves(0, 0, 2)
            if step >= 29:
                done = P * (step - 29)
                quantise_feature(6, done, done + P)
                quantise_feature(7, done, done + P)
            if step == 29:
                invert(0, 0, 2)
                normalise(nc.gpsimd, 0, 0)
                normalise(nc.gpsimd, 0, 1)
            if step == 30:
                score(1, 0, 0, "turn")
                score(1, 0, 1, "turn")
                add_halves(0, 2, 4)

        split_0, split_1 = 256, 704
        invert(0, 2, 4)
        score(1, 1, 0, "z1")
        score(1, 1, 1, "z1")
        quantise_feature(6, 384, 512)
        quantise_feature(7, 384, 512)
        for t, ring in ((2, "turn"), (3, "z1")):
            for h in range(2):
                score(1, t, h, ring)
        normalise(nc.vector, 0, 2)
        normalise(nc.vector, 0, 3)
        add_halves(1, 0, 2)
        group_out("vector", 0, 0, 4, 0, split_0)
        invert(1, 0, 2)
        group_out("scalar", 0, 0, 4, split_0, 512)
        group_out("scalar", 0, 0, 4, 512, ROWS)
        normalise(nc.vector, 1, 0)
        normalise(nc.vector, 1, 1)
        group_out("vector", 1, 0, 2, 0, ROWS)
        add_halves(1, 2, 4)
        quantise_out(0, 0, 512)
        invert(1, 2, 4)
        normalise(nc.vector, 1, 2)
        normalise(nc.vector, 1, 3)
        quantise_out(0, 512, ROWS)
        group_out("vector", 1, 2, 4, 0, 512)
        group_out("scalar", 1, 2, 4, split_1, ROWS)
        group_out("vector", 1, 2, 4, 512, split_1)
        quantise_out(1, 0, 512)
        quantise_out(1, 512, ROWS)
        for Q in range(4):
            nc.scalar.dma_start(
                out=out_2[:, 4 * Q : 4 * Q + 4, :].rearrange("g q m -> q g m").bitcast(I32),
                in_=o_scales[32 * Q : 32 * Q + 4, :, :].bitcast(I32),
            )
